import numpy as np, ml_dtypes
CORES = [16,18,20,22]
N = 4
BF = ml_dtypes.bfloat16
def gentries(a):
    return np.ascontiguousarray(a.reshape(8, 16, -1).transpose(0, 2, 1)).reshape(8, -1)
def gtable(e):
    e = np.asarray(e); return np.ascontiguousarray(e.reshape(8, -1, 16).transpose(0, 2, 1)).reshape(128, -1).astype(np.int32)
R, L, W, RO = 256, 16, 8192, 5
H, SP = L // 2, W // R
def parts(rng):
    X = (rng.integers(0, 256, (N, 8, 16, W)) * rng.integers(64, 257, (N, 8, 1, W))) >> 8
    A = rng.integers(0, W, (N, 8, R, L))
    z = np.maximum(rng.integers(0, 256, (N, 8, 16, R)), rng.integers(0, 256, (N, 8, 1, R)) * rng.integers(0, 2, (N, 8, 1, R)))
    w = rng.integers(0, 256, (N, 8, 16)); T = np.exp2(4 + 5.5 * rng.random((N, 8))).astype(np.int64)
    return X, A, z, w, T
def pack(X, A, z, w, T):
    return {"xd": np.ascontiguousarray(X.reshape(N, 128, W)).astype(np.float32).astype(BF), "ra": np.stack([gtable(a.reshape(8, -1)) for a in A]),
            "zu": np.ascontiguousarray(z.reshape(N, 128, R)).astype(np.float32).astype(BF), "wg": np.ascontiguousarray(w.reshape(N, 128, 1)).astype(np.int32),
            "th": np.repeat(T.reshape(N, 8, 1), 16, axis=2).reshape(N, 128, 1).astype(np.int32)}
def setup_inputs(rng):
    return pack(*parts(rng))
def setup_inputs_ties(rng):
    X, A, z, w, T = parts(rng); m = rng.integers(2, 254 // L + 1, (N, 8)); k = np.arange(L)
    at = rng.integers(0, 16, (N, 8, 1, W)); e = rng.integers(-1, 2, (N, 8, 1, W))
    X = m[:, :, None, None] * (1 + np.arange(W) % L) + e * (np.arange(16)[:, None] == at)
    lev = (2 * k[None, :] + ((np.arange(N) // 2) % 2)[:, None]) % L
    A = L * rng.integers(0, W // L, (N, 8, R, L)) + lev[:, None, None, :]
    o = rng.permutation(8); T = m * np.array([16, 16, 32, 32, 0, 0, 16, 16])[o] + np.array([0, 0, 0, 0, 1, 2, 1, -1])[o]
    z = np.where(rng.random((N, 8, 1, R)) < 0.75, 255, z)
    return pack(X, A, z, w, T)
def setup_inputs_near(rng):
    X0, A, z, w, T = parts(rng); o = [int(v) for v in rng.permutation(8)]; q = [int(v) for v in rng.permutation(N)]; p = (q[1] - 1) % N
    T = rng.integers(2049, 4081, (N, 8)); T[:, o[1]] = 4080; T[:, o[2]] = 2049; T[:, o[3]] = 4 * rng.integers(513, 1020, N)
    e = np.array([-1, 0, 1, -1])[np.arange(W) % 4]
    m = np.maximum(4080 - T[:, :, None] - e, 0)[:, :, None, :]; b = m >> 4
    v = rng.integers(-b, b + 1, (N, 8, 8, W))
    X = 255 - np.concatenate([b + v, b - v], axis=2) - (((np.arange(16)[:, None] + rng.integers(0, 16, (N, 8, 1, W))) & 15) < (m & 15)).astype(np.int64)
    z = np.where(rng.random((N, 8, 1, R)) < 0.75, 255, z); z[p] = 255; z[:, o[0]] = 255
    for r in range(N):
        n = 3 * R - 1 if r == p else int(rng.integers(R, 6 * R))
        yes = (rng.permutation(7 * R) < n).reshape(7, R); c = 4 * rng.integers(0, W // 4, (7, R)); i = rng.integers(0, 2, (7, R))
        A[r, o[1:], :, 0] = np.where(yes, c + 1 + i, np.where(rng.random((7, R)) < 0.5, c + 3 * i, (W - 1) * i))
    X[:, o[0]] = np.arange(W) * 256 // W; T[:, o[0]] = rng.integers(1, 17, N); S = W // (H + 1)
    low = ((np.arange(N) // 2) % 2 == 0)[:, None, None]
    A[:, o[0], :, :H] = np.where(low, 0, S * (1 + np.arange(H)) + rng.integers(0, S // 2, (N, R, H)))
    X[q[0]] = X0[q[0]]; X[q[0], :, :, 31::32] = 255; T[q[0]] = 4080
    for g in range(8):
        f = int(rng.integers(0, 16)); X[q[0], g, f] = np.minimum(X[q[0], g, f], 254)
    return pack(X, A, z, w, T)
def setup_inputs_corners(rng):
    X, A, z, w, T = parts(rng); o = [int(v) for v in rng.permutation(8)]; q = rng.permutation(N)
    A[:, o[0]] = A[:, o[0], :, :1].copy(); T[:, o[0]] = 1
    A[:, o[1]] = rng.choice(np.array([0, W - 1]), (N, R, L))
    z[:, o[2], :, ::2] = 0; z[:, o[2], :, 1::4] = 255; T[:, o[2]] = np.arange(N) % 2
    X[:, o[3], :, ::3] = 255; z[:, o[3]] = 255; T[:, o[3]] = 4080
    w[:, o[4]] = 0
    w[:, o[5]] = 255; z[:, o[5]] = 255; X[:, o[5]] = np.where(rng.random((N, 1, W)) < 0.5, 255, X[:, o[5]])
    A[:, o[6]] = A[0, o[6], 0].copy()
    A[:, o[7]] = np.sort(A[:, o[7]], axis=-1); X[:, o[7]] = np.arange(W) * 240 // W + rng.integers(0, 16, (N, 16, W)); z[:, o[7]] = 255; T[:, o[7]] = 1
    T[q[0]] = 0; T[q[1]] = 4080
    return pack(X, A, z, w, T)
def setup_inputs_ends(rng):
    c = rng.integers(0, 3, (N, 8, 1, W)); X = 255 * np.where(c == 2, rng.integers(0, 2, (N, 8, 16, W)), c)
    X[:, 7, :, W - 1] = 255; X[:, 7, :, 0] = 0; X[:, 3, :, W - 1] = 0; X[:, 3, :, 0] = 255
    p = rng.random((N, 8, R, L)); A = np.where(p < 0.4, 0, np.where(p < 0.8, W - 1, rng.integers(0, W, (N, 8, R, L))))
    c = rng.integers(0, 4, (N, 8, 1, R)); z = 255 * np.where(c == 3, rng.integers(0, 2, (N, 8, 16, R)), (c > 0).astype(np.int64))
    c = rng.integers(0, 3, (N, 8, 1)); w = 255 * np.where(c == 2, rng.integers(0, 2, (N, 8, 16)), c)
    w[:, 7] = 255; w[:, 0, 0] = 0; w[:, 0, 15] = 255
    T = 4080 * rng.integers(0, 2, (N, 8)); T[:, 7] = 4080; T[:, 0] = 0; T[0, 1:7] = 0
    z[:, 7, :, R - 2:] = 255; z[:, 0, :, 0] = 0
    A[:, 7, R - 2, 0] = W - 1; A[:, 7, R - 1] = 0
    A[(np.arange(N) // 2) % 2 == 1, 7, R - 1, H - 1] = W - 1
    return pack(X, A, z, w, T)
def setup_inputs_spread(rng):
    X, A, z, w, T = parts(rng)
    X = (np.exp2(8 * rng.random((N, 8, 1, W))) * rng.random((N, 8, 16, W)) * (rng.random((N, 8, 1, W)) > 0.0625)).astype(np.int64)
    A = np.minimum((W * rng.random((N, 8, R, L)) ** rng.choice(np.array([1.0, 2.0, 6.0]), (N, 8, R, 1))).astype(np.int64), W - 1)
    z = np.where(rng.random((N, 8, 1, R)) < 0.5, z, (np.exp2(8 * rng.random((N, 8, 1, R))) * rng.random((N, 8, 16, R))).astype(np.int64))
    w = np.minimum(np.exp2(8 * rng.random((N, 8, 16))).astype(np.int64) - rng.integers(0, 2, (N, 8, 16)), 255)
    T = np.minimum(np.exp2(12 * rng.random((N, 8))).astype(np.int64) - 1, 4080)
    return pack(X, A, z, w, T)
def check_inputs(d):
    bad = []
    for k, lo, hi in (("xd", 0, 255), ("ra", 0, W - 1), ("zu", 0, 255), ("wg", 0, 255), ("th", 0, 4080)):
        v = np.asarray(d[k]).astype(np.float64)
        if not (np.min(v) >= lo and np.max(v) <= hi): bad.append("range of " + k)
        elif np.any(v != np.floor(v)): bad.append("whole numbers of " + k)
    v = np.asarray(d["th"]).reshape(-1, 16)
    if np.any(v != v[:, :1]): bad.append("th alike in a group")
    return bad
def reference(xd, ra, zu, wg, th):
    X = xd.astype(np.float32).astype(np.int64).reshape(N, 8, 16, W); z = zu.astype(np.float32).astype(np.int64).reshape(N, 8, 16, R)
    A = np.stack([gentries(a) for a in ra]).astype(np.int64).reshape(N, 8, R, L)
    w = wg.astype(np.int64).reshape(N, 8, 16, 1); T = th.astype(np.int64).reshape(N, 8, 16)[:, :, 0]
    turn = [0] * N
    for rnd in range(RO):
        d = 1 + rnd % (N - 2)
        lost = np.zeros((N, 8, R), bool); beaten = np.zeros((N, 8, R), bool); h = np.zeros((N, 8, R), np.int64)
        D1 = np.zeros((N, 8, R, L), np.int64); D2 = np.zeros((N, 8, R, L), np.int64); nz = np.zeros_like(z); nturn = [0] * N
        for q in range(N):
            r = (q - d) % N; s = (q + 1) % N
            C = np.empty((8, R, L), np.int64)
            C[:, :, 0::2] = A[r][:, :, :H]; C[:, :, 1::2] = np.roll(A[s], -turn[q], axis=1)[:, :, :H]
            x = np.take_along_axis(X[q], C.reshape(8, 1, R * L), 2).reshape(8, 16, R, L)
            top = np.maximum.accumulate(np.minimum(x, z[r][:, :, :, None]), axis=3)
            gain = top.copy(); gain[:, :, :, 1:] -= top[:, :, :, :-1]
            click = np.add.reduce(gain, axis=1) >= T[q][:, None, None]
            D = np.take_along_axis(C, np.argsort(~click, axis=2, kind="stable"), 2)
            n = click.astype(np.int64); a = np.add.reduce(n[:, :, 0::2], axis=2); b = np.add.reduce(n[:, :, 1::2], axis=2)
            E = top[:, :, :, L - 1]
            u = np.add.reduce(w[q] * E, axis=1) & 4095
            lost[r] = b > a; D1[r] = D; h[r] = (((u * u) >> 4) + u) & (W - 1)
            beaten[s] = np.roll(a > b, turn[q], axis=1); D2[s] = np.roll(D, turn[q], axis=1)
            nz[r] = np.abs(255 - z[r] - E)
            place = np.arange(R) * SP + (u & (SP - 1))
            np.put_along_axis(X[q], np.repeat(place[:, None, :], 16, axis=1), E, 2)
            nturn[q] = int(np.add.reduce(n.reshape(-1))) % R
        A3 = A.copy(); A3[:, :, :, H - 1] = h
        A = np.where(lost[:, :, :, None], D1, np.where(beaten[:, :, :, None], D2, A3)); z = nz; turn = nturn
    return {"ya": np.stack([gtable(a.reshape(8, -1)) for a in A]).astype(np.float32), "yz": z.reshape(N, 128, R).astype(np.float32)}

@@ -1,0 +1,591 @@
+import numpy as np
+from concourse.bass import DstId, RemoteDMATransfer
+from concourse.mybir import AluOpType as Op, ActivationFunctionType as Fn
+
+N, R, W, RO = 4, 256, 8192, 5
+CFG = {
+    "tails": [(0, 128), (128, 256)],
+    "gath": [(0, 64, "S"), (64, 128, "S"), (128, 192, "S"), (192, 256, "S")],
+    "prep": [(0, 64), (64, 256)],
+    "zs": 5, "clk": "VV", "sgn": "VS",
+    "cut": 4608, "gc": 1.56, "cy": 1.04, "fix": 50.0, "pe": 0.52, "hop": 70.0, "slack": 120.0, "net": 1800.0,
+}
+XP = 1 << 23
+BT = 1 << 22
+ODD = 3 << 21
+KS = 16512
+
+f32, b16, f16, i32, u16 = "float32", "bfloat16", "float16", "int32", "uint16"
+SCRATCH = {}
+def _sb(dt, shape, *names):
+    for n in names:
+        SCRATCH[n] = ("sbuf", [128] + shape, dt)
+_sb(b16, [W], "doc")
+_sb(b16, [R * 16], "gx", "top", "zrep")
+_sb(i32, [R], "ras", "x0", "y0", "ci", "cp", "nn", "a3", "kint", "lo")
+_sb(f32, [RO, R], "fs", "xl", "yl", "zs", "zl", "k3")
+_sb(b16, [RO, R], "us", "ul")
+_sb(f32, [R], "x0f", "y0f", "cf", "rf", "yq", "sp", "t2y", "aa", "uf", "ufl", "kw", "k1", "k2", "k1l", "k2l", "k3l", "kin", "yo")
+_sb(u16, [R], "off")
+_sb(b16, [R], "hib", "sg", "ss", "tt", "dl", "ones")
+_sb(f16, [2 * R], "key")
+_sb(f16, [8, 2 * R], "pb")
+_sb(i32, [1], "wi", "ti")
+_sb(i32, [8], "pc")
+_sb(b16, [144], "g2")
+_sb(b16, [128], "dt1", "dt2")
+_sb(b16, [R], "ee")
+_sb(f32, [32], "col")
+_sb(f32, [8], "cc")
+_sb(i32, [16], "i16", "b32", "vi")
+_sb(i32, [RO, 32], "ix")
+_sb(u16, [RO, 32], "iu")
+_sb(u16, [16], "pl")
+_sb(f32, [144], "q32")
+_sb(b16, [144], "xf", "t1", "g1", "gw", "ww")
+_sb(f16, [144], "plo", "phi", "qlo", "qhi")
+_sb(f32, [128], "i32m", "sa", "saf", "se", "so", "pe", "po", "half")
+_sb(b16, [128], "xh", "gq", "mr", "mh", "mo", "dm", "t2", "t3", "t4", "t5", "t6", "bl", "ib", "in128", "xi", "xif", "mx", "my", "ml", "wv", "wvf",
+    "cy", "ca", "caf", "cpm", "cpf", "ch", "co")
+_sb(f16, [128], "ih", "ih128")
+_sb(b16, [2 * RO, 128], "al")
+_sb(b16, [2, 512], "ry")
+for _k in range(8):
+    SCRATCH["ps%d" % _k] = ("psum", [128, 512], f32)
+SEMAPHORES = ["cV", "cS", "cP", "cG", "snd"] + ["d%d" % _k for _k in range(12)] + ["m%d" % _k for _k in range(32)]
+SZ = {f32: 4, i32: 4, b16: 2, f16: 2, u16: 2}
+ALL = slice(None)
+
+
+def s_(a, b, st=None):
+    return slice(a, b, st)
+
+
+def build(C):
+    ops, lastw, readers, bank = [], {}, {}, {}
+    TAILS, GATH, ZS, GC, CY = C["tails"], C["gath"], C["zs"], C["gc"], C["cy"]
+
+    def A(name, *idx, p=ALL):
+        return (name, idx if idx else (ALL,) * (len(SCRATCH[name][1]) - 1), p)
+
+    def cells(a):
+        sh = SCRATCH[a[0]][1][1:]
+        return np.arange(int(np.prod(sh))).reshape(sh)[a[1]].reshape(-1)
+
+    def add(q, dur, emit, rd, wr, lat=0.0, kind="c", after=(), extra=None):
+        k = len(ops)
+        deps = {}
+        def dep(j, sem=True):
+            if j >= 0 and j != k:
+                deps[j] = deps.get(j, False) or sem
+        for a in rd:
+            for j in np.unique(lastw.setdefault(a[0], np.full(int(np.prod(SCRATCH[a[0]][1][1:])), -1))[cells(a)]):
+                dep(int(j))
+        for a in wr:
+            c = cells(a)
+            lw = lastw.setdefault(a[0], np.full(int(np.prod(SCRATCH[a[0]][1][1:])), -1))
+            for j in np.unique(lw[c]):
+                dep(int(j), not (q == "P" and j >= 0 and ops[int(j)]["q"] == "P"))
+            keep = []
+            for j, m in readers.get(a[0], []):
+                if m[c].any():
+                    dep(j, not (q == "P" and ops[j]["q"] == "P"))
+                    m = m.copy(); m[c] = False
+                if m.any():
+                    keep.append((j, m))
+            readers[a[0]] = keep
+            lw[c] = k
+        for a in rd:
+            m = np.zeros(len(lastw[a[0]]), bool); m[cells(a)] = True
+            readers.setdefault(a[0], []).append((k, m))
+        for nm in set(a[0] for a in list(rd) + list(wr) if a[0][:2] == "ps"):
+            b = bank.setdefault(nm, {"q": None, "run": [], "prev": []})
+            if b["q"] != q:
+                b["prev"], b["run"], b["q"] = b["run"], [], q
+            for j in b["prev"]:
+                dep(j)
+            if q == "P" and b["run"]:
+                dep(b["run"][-1], False)
+            b["run"].append(k)
+        for j in after:
+            dep(j, False)
+        ops.append({"q": q, "dur": dur, "lat": lat, "emit": emit, "deps": deps, "kind": kind, "x": extra})
+        return k
+
+    def n_of(a):
+        return len(cells(a))
+
+    def two(*aps):
+        return all(SZ[SCRATCH[a[0]][2]] == 2 for a in aps)
+
+    def vdur(n, c):
+        return C["fix"] + max(64, n * c) * CY
+
+    def isap(x):
+        return isinstance(x, tuple)
+
+    def ts(out, in0, s1, op0, s2=None, op1=None, ind=None):
+        rd = [in0] + [x for x in (s1, s2) if isap(x)] + ([ind] if ind else [])
+        c = GC if ind else (0.5 if two(out, in0) else 1)
+        return add("V", vdur(n_of(out), c), ("ts", out, in0, s1, s2, op0, op1, ind), rd, [out])
+
+    def tt(out, in0, in1, op, ind=None):
+        c = 1 if "ps" in (in0[0][:2], in1[0][:2]) else 2
+        return add("V", vdur(n_of(out), c), ("tt", out, in0, in1, op, ind), [in0, in1] + ([ind] if ind else []), [out])
+
+    def cp(out, in_, ind=None, oind=None):
+        c = GC if ind else (3.5 if oind else (0.5 if two(out, in_) else 1))
+        n = n_of(in_) if oind else n_of(out)
+        return add("V", vdur(n, c), ("cp", out, in_, ind, oind), [in_] + [x for x in (ind, oind) if x], [out])
+
+    def ms(out, v):
+        return add("V", vdur(n_of(out), 0.5 if two(out) else 1), ("ms", out, v), [], [out])
+
+    def act(out, in_, fn, bias=0.0, scale=1.0, acc=None, ind=None):
+        rd = [in_] + [x for x in (bias, scale) if isap(x)] + ([ind] if ind else [])
+        return add("S", 15 + vdur(n_of(out), GC if ind else 1) + (20 if acc else 0),
+                   ("act", out, in_, fn, bias, scale, acc, ind), rd, [out] + ([acc] if acc else []))
+
+    def mm(out, lhsT, rhs, start, stop):
+        c = 4 if SCRATCH[rhs[0]][2] == f32 else 1
+        return add("P", 10 + max(64, n_of(rhs)) * c * C["pe"], ("mm", out, lhsT, rhs, start, stop), [lhsT, rhs], [out], lat=60)
+
+    def iota(out, pat, base, cm):
+        return add("G", 130 + 2 * n_of(out) * CY, ("iota", out, pat, base, cm), [], [out])
+
+    nd = [0]
+    def load(q, out, src, lat, after=()):
+        nd[0] += 1
+        return add(q, 60, ("load", out, src), [], [out], lat=lat, kind="d", extra="d%d" % (nd[0] - 1), after=after)
+
+    def store(q, dst, src):
+        nd[0] += 1
+        return add(q, 60, ("store", dst, src), [src], [], lat=2000, kind="d", extra="d%d" % (nd[0] - 1))
+
+    nm = [0]
+    def send(src, dsts):
+        nm[0] += 1
+        sem = "m%d" % (nm[0] - 1)
+        k = add("G", 500, ("send", src, dsts, sem), [src], [], kind="s")
+        by = n_of(src) * SZ[SCRATCH[src[0]][2]]
+        add("R", 0, None, [], [d[1] for d in dsts], lat=C["net"] + len(dsts) * 8 * (40 + by / 16.0), kind="r", after=[k], extra=(sem, 16 * len(dsts)))
+        return k
+
+    col = lambda k: A("col", s_(k, k + 1))
+    cc = lambda k: A("cc", s_(k, k + 1))
+    pc = lambda k: A("pc", s_(k, k + 1))
+    win = lambda name, sh: A(name, s_(16 - sh, 144 - sh))
+    K33 = slice(0, 33)
+
+    l1 = load("Y", A("ras"), ("ra", None), 1800)
+    l2 = load("S", A("us", 0, ALL), ("zu", None), 1800)
+    l3 = load("Y", A("doc", s_(0, C["cut"])), ("xd", (0, C["cut"])), 6000, after=[l1])
+    load("S", A("wi"), ("wg", None), 2200, after=[l2])
+    load("S", A("ti"), ("th", None), 2200, after=[l2])
+    i1 = iota(pc(0), [[0, 1]], 0, 1)
+    i2 = iota(A("xf"), [[1, 144]], 0, 0)
+    for nme, pat in (("xh", [[1, 64], [0, 2]]), ("gq", [[1, 8], [0, 16]]), ("mr", [[0, 8], [1, 16]]), ("i16", [[16, 16]])):
+        i2 = iota(A(nme), pat, 0, 0)
+    s0 = send(A("ras"), [(1, A("x0")), (-1, A("y0"))])
+    s1 = send(A("us", 0, ALL), [(1, A("ul", 0, ALL))])
+    i3 = add("G", 20, ("inc", "d11"), [], [], kind="i", after=[s0, s1], extra="d11")
+    load("Y", A("doc", s_(C["cut"], W)), ("xd", (C["cut"], W)), 6000, after=[l3])
+    ops[-1]["deps"][i3] = True
+
+    iota(A("mh"), [[0, 8], [1, 8], [0, 2]], 0, 0)
+    iota(A("mo"), [[0, 64], [1, 2]], 0, 0)
+    ts(pc(1), pc(0), 0x70, Op.bitwise_and)
+    ts(pc(2), pc(0), 15, Op.bitwise_and)
+    ts(pc(3), pc(0), 1, Op.bitwise_and)
+    cp(A("col", s_(0, 4)), A("pc", s_(0, 4)))
+    ts(col(14), col(1), 0.5, Op.mult)
+    ts(col(15), col(1), 1.0 / 16, Op.mult)
+    ts(A("xf"), A("xf"), col(1), Op.subtract)
+    ts(A("xh"), A("xh"), col(14), Op.subtract)
+    J, X16 = col(2), A("xf", s_(0, 128))
+    ts(col(4), J, 8.0, Op.is_ge, 500.0, Op.mult)
+    ts(col(4), col(4), J, Op.add, 2.0, Op.mult)
+    ts(col(5), col(4), 1.0, Op.add)
+    ts(A("se"), X16, col(4), Op.is_equal)
+    ts(A("so"), X16, col(5), Op.is_equal)
+    ts(col(6), J, 14.0, Op.is_ge, 900.0, Op.mult)
+    ts(col(6), col(6), J, Op.add, 0.5, Op.mult)
+    ts(A("sa"), A("xh"), col(6), Op.is_equal)
+    ts(A("saf"), X16, col(6), Op.is_equal)
+    ts(A("ib"), X16, J, Op.is_equal)
+    for nme, v in (("in128", -128.0), ("xi", float(XP)), ("i32m", 1.0), ("t3", 512.0)):
+        act(A(nme), A("ib"), Fn.Copy, scale=v)
+    ts(A("ih"), A("ib"), 1.0, Op.mult)
+    ts(A("ih128"), A("ib"), 128.0, Op.mult)
+    ts(col(7), J, 8.0, Op.is_lt, float(XP), Op.mult)
+    act(A("xif"), A("ib"), Fn.Identity, scale=col(7))
+    for t in range(RO):
+        act(A("al", 2 * t, ALL), A("ib"), Fn.Copy, scale=float((2 * t + 3) << 18))
+        act(A("al", 2 * t + 1, ALL), A("ib"), Fn.Copy, scale=float(-((2 * t + 2) << 18)))
+    ts(A("bl"), A("gq"), col(15), Op.is_equal, 32.0, Op.mult)
+    ts(A("dm"), X16, J, Op.subtract)
+    ts(A("t2"), A("dm"), -1.0, Op.max, 1.0, Op.min)
+    tt(A("mx"), A("t2"), A("bl"), Op.mult)
+    tt(A("my"), A("bl"), A("t3"), Op.subtract)
+    ts(col(8), col(3), 2.0, Op.mult, -1.0, Op.add)
+    act(A("ml"), A("bl"), Fn.Identity, scale=col(8))
+    ts(col(9), col(3), -1.0, Op.mult, 1.0, Op.add)
+    act(A("pe"), A("ib"), Fn.Identity, scale=col(9))
+    act(A("po"), A("ib"), Fn.Identity, scale=col(3))
+    ts(A("t1"), A("xf"), 17.0, Op.is_equal)
+    ts(A("g1"), A("xf"), 16.0, Op.is_equal)
+    tt(A("gw"), A("g1"), A("t1"), Op.subtract)
+    ts(A("gw"), A("gw"), 2.0, Op.mult)
+    act(A("g2"), A("g1"), Fn.Copy, scale=2.0)
+    ts(pc(4), A("ti"), 0xFF0, Op.bitwise_and)
+    ts(pc(5), A("ti"), 15, Op.bitwise_and)
+    ts(col(12), pc(4), -2.0, Op.mult)
+    ts(col(17), pc(5), -2.0, Op.mult, 1.0, Op.add)
+    act(A("dt1"), A("ib"), Fn.Identity, scale=col(12))
+    act(A("dt2"), A("ib"), Fn.Identity, scale=col(17))
+    tt(A("plo"), A("g1"), A("t1"), Op.add)
+    ts(A("phi"), A("plo"), 128.0, Op.mult)
+    cp(A("qlo"), A("g1"))
+    ts(A("qhi"), A("g1"), 128.0, Op.mult)
+    act(A("q32"), A("g1"), Fn.Copy)
+    cp(col(10), A("wi"))
+    ts(col(11), A("wi"), 1.0 / 4096, Op.mult)
+    act(A("ww"), A("g1"), Fn.Identity, scale=col(10))
+    ts(A("wv"), win("plo", 14), col(11), Op.mult)
+    act(A("wvf"), win("g1", 7), Fn.Identity, scale=col(11))
+    ms(A("cc"), 0.0)
+    for k, p, v in ((0, 0, 64.0), (1, 0, 320.0), (1, 32, 160.0), (2, 0, 20480.0), (3, 0, -12288.0), (3, 32, -4.25), (4, 0, -245760.0), (4, 32, -1920.0),
+                    (5, 0, float(ODD))):
+        ms(A("cc", s_(k, k + 1), p=slice(p, p + 1)), v)
+    act(A("cy"), A("mr"), Fn.Identity, scale=cc(0), bias=cc(1))
+    ts(A("t4"), A("mr"), 14.0, Op.is_ge)
+    act(A("ca"), A("t4"), Fn.Identity, scale=cc(2), bias=cc(3))
+    act(A("cpm"), A("mh"), Fn.Identity, scale=cc(4), bias=cc(4))
+    act(A("co"), A("mo"), Fn.Identity, scale=cc(5))
+    ts(A("t5"), A("mr"), 7.0, Op.is_ge)
+    act(A("caf"), A("t5"), Fn.Identity, scale=cc(2), bias=cc(3))
+    act(A("t6"), A("mr"), Fn.Identity, scale=cc(4), bias=cc(4))
+    ts(A("t5"), A("mr"), 8.0, Op.is_lt)
+    tt(A("cpf"), A("t6"), A("t5"), Op.mult)
+    tt(A("ch"), A("t6"), A("cpf"), Op.subtract)
+    ms(A("ones"), 1.0)
+    ms(A("half"), 0.5)
+    for c, (a, b) in enumerate(TAILS):
+        w = b - a
+        ms(A("ry", c, s_(0, 3 * w), p=K33), 0.0)
+        ms(A("ry", c, s_(w, 3 * w), p=slice(0, 1)), 1.0)
+        ms(A("ry", c, s_(2 * w, 3 * w), p=slice(32, 33)), 1.0)
+    ms(A("zrep", s_(15, 16 * R, 16)), 0.0)
+    ts(A("i16"), A("i16"), J, Op.add)
+    ts(A("b32"), A("i16"), 32.0, Op.mult)
+    ts(col(13), J, float(KS), Op.mult, float(1 << 18), Op.add)
+    ts(A("kin"), A("ras"), col(13), Op.add)
+
+    def c33(name):
+        return A(name, p=K33)
+
+    def zrep(t):
+        for k in range(15):
+            if k < ZS:
+                act(A("zrep", s_(k, 16 * R, 16)), A("ul", t, ALL), Fn.Copy)
+            else:
+                cp(A("zrep", s_(k, 16 * R, 16)), A("ul", t, ALL))
+
+    def sign(e, out, in_):
+        if e == "V":
+            ts(out, in_, -1.0, Op.max, 1.0, Op.min)
+        else:
+            act(out, in_, Fn.Sign)
+
+    cp(A("x0f"), A("x0")); cp(A("y0f"), A("y0"))
+    mm(A("ps6", s_(0, R)), A("se"), A("x0f"), True, False)
+    mm(A("ps6", s_(0, R)), A("so"), A("y0f"), False, True)
+    cp(A("off"), A("ps6", s_(0, R)))
+    ts(A("cf"), A("ps6", s_(0, R)), 20480.0, Op.add)
+    zrep(0)
+
+    for t in range(RO):
+        last = t == RO - 1
+        d, d2 = 1 + t % 2, 1 + (t + 1) % 2
+        fo = -d if last else d2 - d
+        so = 1 if last else 1 + d2
+        unroll = A("iu", t - 1, s_(16, 32)) if t else None
+        for (a, b, e) in GATH:
+            o, ind = A("gx", s_(16 * a, 16 * b)), A("off", s_(a, b))
+            if e == "V":
+                cp(o, A("doc"), ind=ind)
+            else:
+                act(o, A("doc"), Fn.Copy, ind=ind)
+        ts(A("hib"), A("cf"), 1.0 / 128, Op.mult, -63.5 / 128, Op.add)
+        for c, (a, b) in enumerate(TAILS):
+            w = b - a
+            yb, vb = "ps%d" % (2 + c), "ps%d" % (4 + c)
+            mm(A(yb, s_(0, 3 * w)), c33("cy"), A("ry", c, s_(0, 3 * w), p=K33), True, False)
+            mm(A(yb, s_(2 * w, 3 * w)), A("i32m"), A("cf", s_(a, b)), False, False)
+            mm(A(yb, s_(w, 2 * w)), A("ib"), A("hib", s_(a, b)), False, False)
+            mm(A(yb, s_(2 * w, 3 * w)), A("in128"), A("hib", s_(a, b)), False, False)
+            mm(A(vb, s_(w, 2 * w)), c33("caf" if last else "ca"), A("ones", s_(0, w), p=K33), True, False)
+            mm(A(vb, s_(w, 2 * w)), A("saf" if last else "sa"), A("cf", s_(a, b)), False, True)
+        for c, (a, b) in enumerate(TAILS):
+            w = b - a
+            gb, yb, vb, pb = "ps%d" % c, "ps%d" % (2 + c), "ps%d" % (4 + c), "ps%d" % (6 + c)
+            ab = s_(a, b)
+            mm(A(gb, s_(0, w)), A("dt1"), A("ones", s_(0, w)), True, False)
+            mm(A(gb, s_(0, w)), A("dt2"), A("ones", s_(0, w)), False, False)
+            mm(A(pb, s_(340, 340 + w)), A("ib"), A("ul", t, ab), True, True)
+            for (a1, b1, e) in GATH:
+                if a <= a1 < b:
+                    v = lambda nme: A(nme, s_(16 * a1, 16 * b1))
+                    add("V", vdur(16 * (b1 - a1), 0.5), ("scan", v("top"), v("gx"), v("zrep")), [v("gx"), v("zrep")], [v("top")])
+                    for k in range(15):
+                        mm(A(gb, s_(a1 - a, b1 - a)), win("gw", k), A("top", s_(16 * a1 + k, 16 * b1, 16)), False, False)
+            E = A("ee", ab)
+            tt(A(pb, s_(170, 170 + w)), A(pb, s_(340, 340 + w)), A("gx", s_(16 * a + 15, 16 * b, 16)), Op.min)
+            tt(E, A(pb, s_(170, 170 + w)), A("top", s_(16 * a + 14, 16 * b, 16)), Op.max)
+            mm(A(gb, s_(0, w)), win("g2", 15), E, False, True)
+            sign(C["clk"][c], A("sg", ab), A(gb, s_(0, w)))
+            mm(A(vb, s_(0, w)), A("wvf" if last else "wv"), E, True, True)
+            mm(A(yb, s_(0, w)), A("mx"), A("sg", ab), False, False)
+            mm(A(yb, s_(w, 2 * w)), A("my"), A("sg", ab), False, False)
+            mm(A(yb, s_(2 * w, 3 * w)), A("my"), A("sg", ab), False, True)
+            mm(A(gb, s_(2 * w, 3 * w)), A("ml"), A("sg", ab), True, True)
+            mm(A(gb, s_(w, 2 * w)), A("ib"), A("ul", t, ab), True, False)
+            mm(A(gb, s_(w, 2 * w)), A("ib"), E, False, True)
+            sign(C["sgn"][c], A("ss", ab), A(gb, s_(2 * w, 3 * w)))
+            act(A("uf", ab) if last else A("us", t + 1, ab), A(gb, s_(w, 2 * w)), Fn.Abs, bias=255.0, scale=-1.0)
+            act(A("dl", ab), A("ss", ab), Fn.Identity, bias=float(-BT), scale=float(-XP - 2 * BT))
+            ts(A("nn", ab), A(vb, s_(0, w)), -2047.5 / 4096, Op.add)
+            tt(A("rf", ab), A(vb, s_(0, w)), A("nn", ab), Op.subtract)
+            act(A("yq", ab), A("rf", ab), Fn.Square, bias=2.0, scale=1024.0)
+            tt(A("tt", ab), A(yb, s_(0, w)), A("sg", ab), Op.mult)
+            kh, kl = s_(2 * a, 2 * a + w), s_(2 * a + w, 2 * b)
+            tt(A("key", kh), A(yb, s_(w, 2 * w)), A("tt", ab), Op.add)
+            tt(A("key", kl), A(yb, s_(2 * w, 3 * w)), A("tt", ab), Op.add)
+            tt(A("a3", ab), A(vb, s_(w, 2 * w)), A("yq", ab), Op.add)
+            P = A(pb, s_(0, w))
+            mm(P, c33("cpf" if last else "cpm"), A("ones", s_(0, w), p=K33), True, False)
+            for j in range(8):
+                ts(A("pb", j, s_(2 * a, 2 * b)), A("key", s_(2 * a, 2 * b)), 128.0 * j, Op.max, 128.0 * (j + 1), Op.min)
+                if j == 4:
+                    mm(P, A("xif" if last else "xi"), A("ss", ab), False, False)
+                mm(P, win("qhi", j) if last else win("phi", 2 * j), A("pb", j, kh), False, False)
+                mm(P, win("qlo", j) if last else win("plo", 2 * j), A("pb", j, kl), False, j == 7)
+            tt(A("fs", t, ab), P, A("a3", ab), Op.max)
+            tt(A("sp", ab) if t else A("zs", t, ab), P, A("dl", ab), Op.add)
+            if c == len(TAILS) - 1:
+                if last:
+                    send(A("uf"), [(fo, A("ufl"))])
+                else:
+                    send(A("us", t + 1, ALL), [(fo, A("ul", t + 1, ALL))])
+        send(A("fs", t, ALL), [(fo, A("xl", t, ALL))] + ([] if last else [(-d - 1, A("yl", t, ALL))]))
+        if t:
+            act(A("zs", t, ALL), A("sp"), Fn.Copy, ind=unroll)
+        send(A("zs", t, ALL), [(so, A("zl", t, ALL))])
+        for kb, al in (("ps2", 2 * t), ("ps3", 2 * t + 1)):
+            for (a, b) in TAILS:
+                w = b - a
+                mm(A(kb, s_(a, b)), A("ih128"), A("key", s_(2 * a, 2 * a + w)), True, False)
+                mm(A(kb, s_(a, b)), A("ih"), A("key", s_(2 * a + w, 2 * b)), False, False)
+                mm(A(kb, s_(a, b)), A("al", al, ALL), A("ss", s_(a, b)), False, True)
+        kacc = A("k1" if d == 1 else "k2")
+        if t < 2:
+            act(kacc, A("ps2", s_(0, R)), Fn.Copy)
+        else:
+            tt(kacc, A("ps2", s_(0, R)), kacc, Op.max)
+        if t == 0:
+            act(A("k3", t, ALL), A("ps3", s_(0, R)), Fn.Copy)
+        else:
+            act(A("kw"), A("ps3", s_(0, R)), Fn.Copy)
+            tt(A("k3", t, ALL), A("kw"), A("k3", t - 1, ALL), Op.max, ind=unroll)
+        if t == RO - 2:
+            send(A("k2"), [(-2, A("k2l"))])
+            tt(A("kin"), A("kin"), A("k2l"), Op.max)
+        if last:
+            send(A("k1"), [(-1, A("k1l"))])
+            send(A("k3", t, ALL), [(1, A("k3l"))])
+            break
+        act(A("tt"), A("sg"), Fn.Copy, acc=col(16))
+        mm(A("ps0", s_(0, 1)), A("half"), col(16), True, True)
+        ts(A("ix", t, s_(0, 16)), A("i16"), A("ps0", s_(0, 1)), Op.add)
+        ts(A("ix", t, s_(16, 32)), A("i16"), A("ps0", s_(0, 1)), Op.subtract)
+        ts(A("ix", t, ALL), A("ix", t, ALL), 255, Op.bitwise_and)
+        cp(A("iu", t, ALL), A("ix", t, ALL))
+        for m in range(16):
+            mm(A("ps1", s_(0, 16)), win("ww", m), A("ee", s_(m, R, 16)), m == 0, m == 15)
+        cp(A("vi"), A("ps1", s_(0, 16)))
+        ts(A("vi"), A("vi"), 31, Op.bitwise_and)
+        tt(A("vi"), A("vi"), A("b32"), Op.add)
+        cp(A("pl"), A("vi"))
+        cp(A("doc"), A("ee"), oind=A("pl"))
+        zrep(t + 1)
+        tt(A("t2y"), A("yl", t, ALL), A("zs", t, ALL), Op.max)
+        act(A("aa"), A("t2y"), Fn.Copy, ind=A("iu", t, s_(0, 16)))
+        B = A("ps6", s_(0, R))
+        mm(B, c33("co"), A("ones", p=K33), True, False)
+        mm(B, A("pe"), A("xl", t, ALL), False, False)
+        mm(B, A("po"), A("aa"), False, True)
+        for (a, b) in C["prep"]:
+            ab = s_(a, b)
+            tt(A("cp", ab), A("ps6", ab), A("zl", t, ab), Op.max)
+            ts(A("ci", ab), A("cp", ab), 8191, Op.bitwise_and)
+            cp(A("off", ab), A("ci", ab))
+        ts(A("cf"), A("ci"), 20480.0, Op.add)
+
+    t = RO - 1
+    store("Y", "yz", A("ufl"))
+    tt(A("ps4", s_(0, R)), A("kin"), A("k1l"), Op.max)
+    tt(A("kint"), A("ps4", s_(0, R)), A("k3l"), Op.max)
+    ts(A("kint"), A("kint"), (1 << 18) - 1, Op.bitwise_and)
+    Hh = A("ps5", s_(0, R))
+    mm(Hh, c33("ch"), A("ones", p=K33), True, False)
+    hb = [A("x0f"), A("y0f"), A("cf"), A("rf"), A("t2y"), A("aa"), A("yl", 4, ALL), A("kw")]
+    for j in range(8, 16):
+        ts(hb[j - 8], A("kint"), float(KS * j), Op.max, float(KS * (j + 1)), Op.min)
+        mm(Hh, win("q32", j), hb[j - 8], False, j == 15)
+    tt(A("lo"), A("xl", t, ALL), A("zl", t, ALL), Op.max)
+    ts(A("lo"), A("lo"), 8191, Op.bitwise_and)
+    tt(A("yo"), Hh, A("lo"), Op.add)
+    store("Y", "ya", A("yo"))
+    return ops
+
+
+def schedule(ops, C):
+    n, hop, slack = len(ops), C["hop"], C["slack"]
+    succ = [[] for _ in range(n)]
+    left = [len(o["deps"]) for o in ops]
+    for k, o in enumerate(ops):
+        for j in o["deps"]:
+            succ[j].append(k)
+    pri = [0.0] * n
+    for k in range(n - 1, -1, -1):
+        pri[k] = ops[k]["dur"] + ops[k]["lat"] + max([pri[j] + hop for j in succ[k]] + [0.0])
+    free, rdy, fin, order = {}, [0.0] * n, [0.0] * n, []
+    cand = [k for k in range(n) if left[k] == 0]
+    while cand:
+        st = {k: max(rdy[k], free.get(ops[k]["q"], 0.0) if ops[k]["q"] != "R" else 0.0) for k in cand}
+        k0 = min(cand, key=lambda k: (st[k], -pri[k]))
+        q = ops[k0]["q"]
+        k = max([j for j in cand if ops[j]["q"] == q and st[j] <= st[k0] + slack], key=lambda j: (pri[j], -j))
+        cand.remove(k); order.append(k)
+        free[q] = st[k] + ops[k]["dur"]
+        fin[k] = free[q] + ops[k]["lat"]
+        ops[k]["st"] = st[k]
+        for j in succ[k]:
+            sem = ops[j]["deps"][k]
+            rdy[j] = max(rdy[j], fin[k] + hop if sem else (free[q] if ops[j]["q"] == "R" else 0.0))
+            left[j] -= 1
+            if left[j] == 0:
+                cand.append(j)
+    return order, max(fin)
+
+
+PLAN = []
+
+
+def rank_program(g, core, T, topo):
+    rank = T.rank_of(core)
+    if rank is None:
+        return
+    if not PLAN:
+        o = build(CFG)
+        PLAN.append(o); PLAN.append(schedule(o, CFG)[0])
+    ops, order = PLAN
+    Q = {"V": g.vector, "S": g.scalar, "P": g.tensor, "G": g, "Y": g.sync}
+    need = set(j for o in ops for j, sem in o["deps"].items() if sem)
+    count, mark, clock, vc = {}, {}, {q: {} for q in Q}, {}
+    sent = [0]
+
+    def ap(a, ind=None):
+        v = T[a[0]][(a[2],) + tuple(a[1])]
+        return v.indirect(ap(ind)) if ind else v
+
+    def sc(x):
+        return ap(x) if isinstance(x, tuple) else x
+
+    def wait(q, sem, n, known):
+        if clock[q].get(sem, 0) < n:
+            Q[q].wait_ge(T.sem[sem], n)
+            clock[q][sem] = n
+        for s, v in known.items():
+            if clock[q].get(s, 0) < v:
+                clock[q][s] = v
+
+    for k in order:
+        o = ops[k]
+        q, e = o["q"], o["emit"]
+        if o["kind"] == "r":
+            mark[k] = o["x"]; vc[k] = {}
+            continue
+        ds = sorted([j for j, sem in o["deps"].items() if sem and ops[j]["kind"] != "s"], key=lambda j: -mark[j][1])
+        for j in ds:
+            wait(q, mark[j][0], mark[j][1], vc[j])
+        w = e[0]
+        if w == "ts":
+            _, out, in0, s1, s2, op0, op1, ind = e
+            ins = g.vector.tensor_scalar(ap(out), ap(in0, ind), sc(s1), sc(s2), op0, op1) if op1 is not None else \
+                g.vector.tensor_scalar(ap(out), ap(in0, ind), sc(s1), None, op0)
+        elif w == "tt":
+            ins = g.vector.tensor_tensor(ap(e[1]), ap(e[2], e[5]), ap(e[3]), e[4])
+        elif w == "cp":
+            ins = g.vector.tensor_copy(ap(e[1], e[4]), ap(e[2], e[3]))
+        elif w == "ms":
+            ins = g.vector.memset(ap(e[1]), e[2])
+        elif w == "scan":
+            ins = g.vector.tensor_tensor_scan(ap(e[1]), ap(e[2]), ap(e[3]), 0.0, Op.max, Op.min)
+        elif w == "act":
+            _, out, in_, fn, bias, scale, acc, ind = e
+            kw = {}
+            if isinstance(bias, tuple) or bias != 0.0:
+                kw["bias"] = sc(bias)
+            if isinstance(scale, tuple) or scale != 1.0:
+                kw["scale"] = sc(scale)
+            if acc:
+                kw["accum_out"] = ap(acc)
+            ins = g.scalar.activation(ap(out), ap(in_, ind), fn, **kw)
+        elif w == "mm":
+            ins = g.tensor.matmul(ap(e[1]), ap(e[2]), ap(e[3]), e[4], e[5])
+        elif w == "iota":
+            if SCRATCH[e[1][0]][2] == i32:
+                ins = g.iota(ap(e[1]), e[2], e[3], e[4])
+            else:
+                ins = g.iota(ap(e[1]), e[2], e[3], e[4], allow_small_or_imprecise_dtypes=True)
+        elif w == "load":
+            src = T[e[2][0]][:] if e[2][1] is None else T[e[2][0]][:, e[2][1][0]:e[2][1][1]]
+            ins = Q[q].dma_start(ap(e[1]), src)
+        elif w == "store":
+            ins = Q[q].dma_start(T[e[1]][:], ap(e[2]))
+        elif w == "inc":
+            g.sem_inc(T.sem[e[1]], 1)
+            mark[k] = (e[1], 1); vc[k] = {}
+            continue
+        else:
+            _, src, dsts, sem = e
+            to = [T.cores[(rank + off) % N] for off, _a in dsts]
+            mask = topo.mask(core, to[0])
+            for c in to[1:]:
+                mask &= topo.mask(core, c)
+            ne = bin(mask).count("1")
+            if len(to) == 1:
+                rid, pid, _s = topo.addr(to[0])
+                g.remote_dma(ap(dsts[0][1]), ap(src), T.sem[sem], T.sem.snd, pid, rid, mask)
+            else:
+                ids = [DstId(rid=topo.addr(c)[0], pnc=topo.addr(c)[1]) for c in to]
+                g.remote_dma_fused([RemoteDMATransfer(dst_ids=ids, dma_engine_mask=mask, remote_sem=T.sem[sem], src=ap(src),
+                                                      dsts=[ap(a) for _o, a in dsts])], local_sem=T.sem.snd)
+            sent[0] += ne
+            continue
+        if o["kind"] == "d":
+            ins.then_inc(T.sem[o["x"]], 16)
+            mark[k] = (o["x"], 16)
+        elif k in need:
+            s = "c" + q
+            count[s] = count.get(s, 0) + 1
+            ins.then_inc(T.sem[s], 1)
+            mark[k] = (s, count[s])
+        vc[k] = dict(clock[q])
+    for k in mark:
+        if ops[k]["kind"] != "c":
+            wait("G", mark[k][0], mark[k][1], {})
+    for s in count:
+        wait("G", s, count[s], {})
+    g.wait_ge(T.sem.snd, sent[0])

@@ -5,14 +5,16 @@ from concourse.mybir import AluOpType as Op, ActivationFunctionType as Fn
 N, R, W, RO = 4, 256, 8192, 5
 CFG = {
     "tails": [(0, 128), (128, 256)],
-    "gath": [(0, 64, "S"), (64, 128, "S"), (128, 192, "S"), (192, 256, "S")],
-    "prep": [(0, 64), (64, 256)],
-    "zs": 5, "clk": "VV", "sgn": "VS",
-    "cut": 4608, "gc": 1.56, "cy": 1.04, "fix": 50.0, "pe": 0.52, "hop": 70.0, "slack": 120.0, "net": 1800.0,
+    "gath": [(0, 64, "V"), (64, 128, "S"), (128, 192, "S"), (192, 256, "S")],
+    "prep": [(0, 128), (128, 256)],
+    "zs": 10, "clk": "VS", "sgn": "SS", "split": 1, "hib": "V", "iters": 6,
+    "cut": 4608, "gc": 1.56, "cy": 0.92, "fix": 45.0, "pe": 0.46, "hop": 60.0, "slack": 30.0, "net": 1800.0, "iss": 500.0,
 }
-XP = 1 << 23
-BT = 1 << 22
-ODD = 3 << 21
+MI = 1 << 20
+XP = 4 * MI
+HI = 4 * MI
+ODD = 6 * MI
+MAGIC = float(3 << 22)
 KS = 16512
 
 f32, b16, f16, i32, u16 = "float32", "bfloat16", "float16", "int32", "uint16"
@@ -22,7 +24,7 @@ def _sb(dt, shape, *names):
         SCRATCH[n] = ("sbuf", [128] + shape, dt)
 _sb(b16, [W], "doc")
 _sb(b16, [R * 16], "gx", "top", "zrep")
-_sb(i32, [R], "ras", "x0", "y0", "ci", "cp", "nn", "a3", "kint", "lo")
+_sb(i32, [R], "ras", "x0", "y0", "ci", "cp", "kint", "lo")
 _sb(f32, [RO, R], "fs", "xl", "yl", "zs", "zl", "k3")
 _sb(b16, [RO, R], "us", "ul")
 _sb(f32, [R], "x0f", "y0f", "cf", "rf", "yq", "sp", "t2y", "aa", "uf", "ufl", "kw", "k1", "k2", "k1l", "k2l", "k3l", "kin", "yo")
@@ -33,8 +35,10 @@ _sb(f16, [8, 2 * R], "pb")
 _sb(i32, [1], "wi", "ti")
 _sb(i32, [8], "pc")
 _sb(b16, [144], "g2")
-_sb(b16, [128], "dt1", "dt2")
-_sb(b16, [R], "ee")
+_sb(b16, [128], "dt1", "dt2", "in1", "cv")
+_sb(b16, [R], "ee", "nb")
+_sb(i32, [R], "a3")
+_sb(f32, [R], "xm")
 _sb(f32, [32], "col")
 _sb(f32, [8], "cc")
 _sb(i32, [16], "i16", "b32", "vi")
@@ -44,9 +48,9 @@ _sb(u16, [16], "pl")
 _sb(f32, [144], "q32")
 _sb(b16, [144], "xf", "t1", "g1", "gw", "ww")
 _sb(f16, [144], "plo", "phi", "qlo", "qhi")
-_sb(f32, [128], "i32m", "sa", "saf", "se", "so", "pe", "po", "half")
-_sb(b16, [128], "xh", "gq", "mr", "mh", "mo", "dm", "t2", "t3", "t4", "t5", "t6", "bl", "ib", "in128", "xi", "xif", "mx", "my", "ml", "wv", "wvf",
-    "cy", "ca", "caf", "cpm", "cpf", "ch", "co")
+_sb(f32, [128], "i32m", "sa", "saf", "se", "so", "half")
+_sb(b16, [128], "xh", "gq", "mr", "mh", "dm", "t2", "t3", "t4", "t5", "t6", "bl", "ib", "in128", "xi", "xif", "mx", "my", "ml", "wv", "wvf",
+    "cy", "ca", "caf", "cpm", "cpf", "ch")
 _sb(f16, [128], "ih", "ih128")
 _sb(b16, [2 * RO, 128], "al")
 _sb(b16, [2, 512], "ry")
@@ -166,7 +170,7 @@ def build(C):
     def send(src, dsts):
         nm[0] += 1
         sem = "m%d" % (nm[0] - 1)
-        k = add("G", 500, ("send", src, dsts, sem), [src], [], kind="s")
+        k = add("G", C["iss"], ("send", src, dsts, sem), [src], [], kind="s")
         by = n_of(src) * SZ[SCRATCH[src[0]][2]]
         add("R", 0, None, [], [d[1] for d in dsts], lat=C["net"] + len(dsts) * 8 * (40 + by / 16.0), kind="r", after=[k], extra=(sem, 16 * len(dsts)))
         return k
@@ -175,7 +179,7 @@ def build(C):
     cc = lambda k: A("cc", s_(k, k + 1))
     pc = lambda k: A("pc", s_(k, k + 1))
     win = lambda name, sh: A(name, s_(16 - sh, 144 - sh))
-    K33 = slice(0, 33)
+    K33, K65 = slice(0, 33), slice(0, 65)
 
     l1 = load("Y", A("ras"), ("ra", None), 1800)
     l2 = load("S", A("us", 0, ALL), ("zu", None), 1800)
@@ -193,7 +197,6 @@ def build(C):
     ops[-1]["deps"][i3] = True
 
     iota(A("mh"), [[0, 8], [1, 8], [0, 2]], 0, 0)
-    iota(A("mo"), [[0, 64], [1, 2]], 0, 0)
     ts(pc(1), pc(0), 0x70, Op.bitwise_and)
     ts(pc(2), pc(0), 15, Op.bitwise_and)
     ts(pc(3), pc(0), 1, Op.bitwise_and)
@@ -213,7 +216,7 @@ def build(C):
     ts(A("sa"), A("xh"), col(6), Op.is_equal)
     ts(A("saf"), X16, col(6), Op.is_equal)
     ts(A("ib"), X16, J, Op.is_equal)
-    for nme, v in (("in128", -128.0), ("xi", float(XP)), ("i32m", 1.0), ("t3", 512.0)):
+    for nme, v in (("in128", -128.0), ("xi", float(XP)), ("i32m", 1.0), ("in1", -1.0), ("t3", 512.0)):
         act(A(nme), A("ib"), Fn.Copy, scale=v)
     ts(A("ih"), A("ib"), 1.0, Op.mult)
     ts(A("ih128"), A("ib"), 128.0, Op.mult)
@@ -230,8 +233,8 @@ def build(C):
     ts(col(8), col(3), 2.0, Op.mult, -1.0, Op.add)
     act(A("ml"), A("bl"), Fn.Identity, scale=col(8))
     ts(col(9), col(3), -1.0, Op.mult, 1.0, Op.add)
-    act(A("pe"), A("ib"), Fn.Identity, scale=col(9))
-    act(A("po"), A("ib"), Fn.Identity, scale=col(3))
+    ts(col(18), col(9), float(HI), Op.mult)
+    ts(col(19), col(9), float(-HI - ODD), Op.mult, float(ODD), Op.add)
     ts(A("t1"), A("xf"), 17.0, Op.is_equal)
     ts(A("g1"), A("xf"), 16.0, Op.is_equal)
     tt(A("gw"), A("g1"), A("t1"), Op.subtract)
@@ -253,22 +256,22 @@ def build(C):
     act(A("ww"), A("g1"), Fn.Identity, scale=col(10))
     ts(A("wv"), win("plo", 14), col(11), Op.mult)
     act(A("wvf"), win("g1", 7), Fn.Identity, scale=col(11))
+    ms(A("ones"), 1.0)
     ms(A("cc"), 0.0)
-    for k, p, v in ((0, 0, 64.0), (1, 0, 320.0), (1, 32, 160.0), (2, 0, 20480.0), (3, 0, -12288.0), (3, 32, -4.25), (4, 0, -245760.0), (4, 32, -1920.0),
-                    (5, 0, float(ODD))):
+    for k, p, v in ((0, 0, 64.0), (1, 0, 320.0), (1, 32, 160.0), (2, 0, 20480.0), (3, 0, -20480.0), (3, 32, -4.25), (4, 0, -245760.0), (4, 32, -1920.0),
+                    (6, 0, -0.5), (6, 32, 2.0 ** -13), (7, 0, -245760.0), (7, 32, -1920.0), (7, 64, float(-MI))):
         ms(A("cc", s_(k, k + 1), p=slice(p, p + 1)), v)
     act(A("cy"), A("mr"), Fn.Identity, scale=cc(0), bias=cc(1))
     ts(A("t4"), A("mr"), 14.0, Op.is_ge)
     act(A("ca"), A("t4"), Fn.Identity, scale=cc(2), bias=cc(3))
-    act(A("cpm"), A("mh"), Fn.Identity, scale=cc(4), bias=cc(4))
-    act(A("co"), A("mo"), Fn.Identity, scale=cc(5))
+    act(A("cpm"), A("mh"), Fn.Identity, scale=cc(4), bias=cc(7))
+    act(A("cv"), A("ones", s_(0, 128)), Fn.Identity, scale=cc(6))
     ts(A("t5"), A("mr"), 7.0, Op.is_ge)
     act(A("caf"), A("t5"), Fn.Identity, scale=cc(2), bias=cc(3))
-    act(A("t6"), A("mr"), Fn.Identity, scale=cc(4), bias=cc(4))
+    act(A("t6"), A("mr"), Fn.Identity, scale=cc(4), bias=cc(7))
     ts(A("t5"), A("mr"), 8.0, Op.is_lt)
     tt(A("cpf"), A("t6"), A("t5"), Op.mult)
     tt(A("ch"), A("t6"), A("cpf"), Op.subtract)
-    ms(A("ones"), 1.0)
     ms(A("half"), 0.5)
     for c, (a, b) in enumerate(TAILS):
         w = b - a
@@ -316,7 +319,10 @@ def build(C):
                 cp(o, A("doc"), ind=ind)
             else:
                 act(o, A("doc"), Fn.Copy, ind=ind)
-        ts(A("hib"), A("cf"), 1.0 / 128, Op.mult, -63.5 / 128, Op.add)
+        if C["hib"] == "V":
+            ts(A("hib"), A("cf"), 1.0 / 128, Op.mult, -63.5 / 128, Op.add)
+        else:
+            act(A("hib"), A("cf"), Fn.Identity, bias=-63.5 / 128, scale=1.0 / 128)
         for c, (a, b) in enumerate(TAILS):
             w = b - a
             yb, vb = "ps%d" % (2 + c), "ps%d" % (4 + c)
@@ -344,31 +350,34 @@ def build(C):
             tt(E, A(pb, s_(170, 170 + w)), A("top", s_(16 * a + 14, 16 * b, 16)), Op.max)
             mm(A(gb, s_(0, w)), win("g2", 15), E, False, True)
             sign(C["clk"][c], A("sg", ab), A(gb, s_(0, w)))
-            mm(A(vb, s_(0, w)), A("wvf" if last else "wv"), E, True, True)
+            mm(A(vb, s_(0, w)), c33("cv"), A("ones", s_(0, w), p=K33), True, False)
+            mm(A(vb, s_(0, w)), A("wvf" if last else "wv"), E, False, True)
+            mm(A(vb, s_(2 * w, 3 * w)), A("ib"), A("ul", t, ab), True, False)
+            mm(A(vb, s_(2 * w, 3 * w)), A("ib"), E, False, True)
+            act(A("uf", ab) if last else A("us", t + 1, ab), A(vb, s_(2 * w, 3 * w)), Fn.Abs, bias=255.0, scale=-1.0)
             mm(A(yb, s_(0, w)), A("mx"), A("sg", ab), False, False)
             mm(A(yb, s_(w, 2 * w)), A("my"), A("sg", ab), False, False)
             mm(A(yb, s_(2 * w, 3 * w)), A("my"), A("sg", ab), False, True)
             mm(A(gb, s_(2 * w, 3 * w)), A("ml"), A("sg", ab), True, True)
-            mm(A(gb, s_(w, 2 * w)), A("ib"), A("ul", t, ab), True, False)
-            mm(A(gb, s_(w, 2 * w)), A("ib"), E, False, True)
             sign(C["sgn"][c], A("ss", ab), A(gb, s_(2 * w, 3 * w)))
-            act(A("uf", ab) if last else A("us", t + 1, ab), A(gb, s_(w, 2 * w)), Fn.Abs, bias=255.0, scale=-1.0)
-            act(A("dl", ab), A("ss", ab), Fn.Identity, bias=float(-BT), scale=float(-XP - 2 * BT))
-            ts(A("nn", ab), A(vb, s_(0, w)), -2047.5 / 4096, Op.add)
-            tt(A("rf", ab), A(vb, s_(0, w)), A("nn", ab), Op.subtract)
-            act(A("yq", ab), A("rf", ab), Fn.Square, bias=2.0, scale=1024.0)
+            act(A("dl", ab), A("ss", ab), Fn.Identity, bias=float(-MI), scale=float(-8 * MI))
+            act(A("rf", ab), A(vb, s_(0, w)), Fn.Identity, bias=MAGIC)
+            act(A("nb", ab), A("rf", ab), Fn.Identity, bias=-MAGIC)
+            mm(A(vb, s_(0, w)), A("wvf" if last else "wv"), E, True, False)
+            mm(A(vb, s_(0, w)), A("in1"), A("nb", ab), False, True)
+            act(A("yq", ab), A(vb, s_(0, w)), Fn.Square, bias=2.0, scale=1024.0)
+            tt(A("a3", ab), A(vb, s_(w, 2 * w)), A("yq", ab), Op.add)
             tt(A("tt", ab), A(yb, s_(0, w)), A("sg", ab), Op.mult)
             kh, kl = s_(2 * a, 2 * a + w), s_(2 * a + w, 2 * b)
             tt(A("key", kh), A(yb, s_(w, 2 * w)), A("tt", ab), Op.add)
             tt(A("key", kl), A(yb, s_(2 * w, 3 * w)), A("tt", ab), Op.add)
-            tt(A("a3", ab), A(vb, s_(w, 2 * w)), A("yq", ab), Op.add)
             P = A(pb, s_(0, w))
-            mm(P, c33("cpf" if last else "cpm"), A("ones", s_(0, w), p=K33), True, False)
+            mm(P, A("cpf" if last else "cpm", p=K65), A("ones", s_(0, w), p=K65), True, False)
             for j in range(8):
                 ts(A("pb", j, s_(2 * a, 2 * b)), A("key", s_(2 * a, 2 * b)), 128.0 * j, Op.max, 128.0 * (j + 1), Op.min)
-                if j == 4:
-                    mm(P, A("xif" if last else "xi"), A("ss", ab), False, False)
                 mm(P, win("qhi", j) if last else win("phi", 2 * j), A("pb", j, kh), False, False)
+                if j == 7:
+                    mm(P, A("xif" if last else "xi"), A("ss", ab), False, False)
                 mm(P, win("qlo", j) if last else win("plo", 2 * j), A("pb", j, kl), False, j == 7)
             tt(A("fs", t, ab), P, A("a3", ab), Op.max)
             tt(A("sp", ab) if t else A("zs", t, ab), P, A("dl", ab), Op.add)
@@ -377,7 +386,11 @@ def build(C):
                     send(A("uf"), [(fo, A("ufl"))])
                 else:
                     send(A("us", t + 1, ALL), [(fo, A("ul", t + 1, ALL))])
-        send(A("fs", t, ALL), [(fo, A("xl", t, ALL))] + ([] if last else [(-d - 1, A("yl", t, ALL))]))
+        if C["split"] and not last:
+            send(A("fs", t, ALL), [(-d - 1, A("yl", t, ALL))])
+            send(A("fs", t, ALL), [(fo, A("xl", t, ALL))])
+        else:
+            send(A("fs", t, ALL), [(fo, A("xl", t, ALL))] + ([] if last else [(-d - 1, A("yl", t, ALL))]))
         if t:
             act(A("zs", t, ALL), A("sp"), Fn.Copy, ind=unroll)
         send(A("zs", t, ALL), [(so, A("zl", t, ALL))])
@@ -418,15 +431,14 @@ def build(C):
         cp(A("pl"), A("vi"))
         cp(A("doc"), A("ee"), oind=A("pl"))
         zrep(t + 1)
-        tt(A("t2y"), A("yl", t, ALL), A("zs", t, ALL), Op.max)
-        act(A("aa"), A("t2y"), Fn.Copy, ind=A("iu", t, s_(0, 16)))
-        B = A("ps6", s_(0, R))
-        mm(B, c33("co"), A("ones", p=K33), True, False)
-        mm(B, A("pe"), A("xl", t, ALL), False, False)
-        mm(B, A("po"), A("aa"), False, True)
-        for (a, b) in C["prep"]:
+        act(A("t2y"), A("zs", t, ALL), Fn.Identity, scale=col(3), bias=col(18), ind=A("iu", t, s_(0, 16)))
+        for c, (a, b) in enumerate(C["prep"]):
             ab = s_(a, b)
-            tt(A("cp", ab), A("ps6", ab), A("zl", t, ab), Op.max)
+            B = A("ps%d" % (6 + c), s_(0, b - a))
+            tt(A("aa", ab), A("yl", t, ALL), A("t2y", ab), Op.max, ind=A("iu", t, s_(a // 16, b // 16)))
+            act(A("xm", ab), A("xl", t, ab), Fn.Identity, scale=col(9), bias=col(19))
+            tt(B, A("aa", ab), A("xm", ab), Op.add)
+            tt(A("cp", ab), B, A("zl", t, ab), Op.max)
             ts(A("ci", ab), A("cp", ab), 8191, Op.bitwise_and)
             cp(A("off", ab), A("ci", ab))
         ts(A("cf"), A("ci"), 20480.0, Op.add)
@@ -449,34 +461,58 @@ def build(C):
     return ops
 
 
-def schedule(ops, C):
+def one_pass(ops, pred, succ, pri, C, back):
     n, hop, slack = len(ops), C["hop"], C["slack"]
-    succ = [[] for _ in range(n)]
-    left = [len(o["deps"]) for o in ops]
-    for k, o in enumerate(ops):
-        for j in o["deps"]:
-            succ[j].append(k)
-    pri = [0.0] * n
-    for k in range(n - 1, -1, -1):
-        pri[k] = ops[k]["dur"] + ops[k]["lat"] + max([pri[j] + hop for j in succ[k]] + [0.0])
-    free, rdy, fin, order = {}, [0.0] * n, [0.0] * n, []
-    cand = [k for k in range(n) if left[k] == 0]
-    while cand:
-        st = {k: max(rdy[k], free.get(ops[k]["q"], 0.0) if ops[k]["q"] != "R" else 0.0) for k in cand}
-        k0 = min(cand, key=lambda k: (st[k], -pri[k]))
-        q = ops[k0]["q"]
-        k = max([j for j in cand if ops[j]["q"] == q and st[j] <= st[k0] + slack], key=lambda j: (pri[j], -j))
-        cand.remove(k); order.append(k)
-        free[q] = st[k] + ops[k]["dur"]
-        fin[k] = free[q] + ops[k]["lat"]
-        ops[k]["st"] = st[k]
-        for j in succ[k]:
-            sem = ops[j]["deps"][k]
-            rdy[j] = max(rdy[j], fin[k] + hop if sem else (free[q] if ops[j]["q"] == "R" else 0.0))
+    left = [len(p) for p in pred]
+    free, rdy, fin, st0, order = {}, [0.0] * n, [0.0] * n, [0.0] * n, []
+    cand = {}
+    for k in range(n):
+        if left[k] == 0:
+            cand.setdefault(ops[k]["q"], []).append(k)
+    for _ in range(n):
+        bq, bt = None, 1e30
+        for q, l in cand.items():
+            if l:
+                t = max(min([rdy[j] for j in l]), free.get(q, 0.0) if q != "R" else 0.0)
+                if t < bt:
+                    bq, bt = q, t
+        l = cand[bq]
+        k = max([j for j in l if rdy[j] <= bt + slack], key=lambda j: pri[j])
+        l.remove(k); order.append(k)
+        st0[k] = max(rdy[k], free.get(bq, 0.0) if bq != "R" else 0.0)
+        free[bq] = e = st0[k] + ops[k]["dur"]
+        fin[k] = e + (0.0 if back else ops[k]["lat"])
+        for j, sem in succ[k]:
+            if sem:
+                v = fin[k] + hop + (ops[j]["lat"] if back else 0.0)
+            else:
+                v = e if ops[k if back else j]["q"] == "R" else 0.0
+            rdy[j] = max(rdy[j], v)
             left[j] -= 1
             if left[j] == 0:
-                cand.append(j)
-    return order, max(fin)
+                cand.setdefault(ops[j]["q"], []).append(j)
+    return order, max(fin), st0, fin
+
+
+def schedule(ops, C):
+    n = len(ops)
+    pred = [list(o["deps"].items()) for o in ops]
+    succ = [[] for _ in range(n)]
+    for k in range(n):
+        for j, sem in pred[k]:
+            succ[j].append((k, sem))
+    pri = [0.0] * n
+    for k in range(n - 1, -1, -1):
+        pri[k] = ops[k]["dur"] + ops[k]["lat"] + max([pri[j] + C["hop"] for j, _s in succ[k]] + [0.0])
+    best = None
+    for _ in range(C["iters"]):
+        order, t, st, fin = one_pass(ops, pred, succ, pri, C, False)
+        if best is None or t < best[1]:
+            best = (order, t, st)
+        pri = one_pass(ops, succ, pred, fin, C, True)[3]
+    for k in range(n):
+        ops[k]["st"] = best[2][k]
+    return best[0], best[1]
 
 
 PLAN = []

@@ -5,17 +5,23 @@ from concourse.mybir import AluOpType as Op, ActivationFunctionType as Fn
 N, R, W, RO = 4, 256, 8192, 5
 CFG = {
     "tails": [(0, 128), (128, 256)],
-    "gath": [(0, 64, "V"), (64, 128, "S"), (128, 192, "S"), (192, 256, "S")],
-    "prep": [(0, 128), (128, 256)],
-    "zs": 10, "clk": "VS", "sgn": "SS", "split": 1, "hib": "V", "iters": 6,
-    "cut": 4608, "gc": 1.56, "cy": 0.92, "fix": 45.0, "pe": 0.46, "hop": 60.0, "slack": 30.0, "net": 1800.0, "iss": 500.0,
+    "gath": [(32 * _k, 32 * _k + 32, _e) for _k, _e in enumerate("SVSSVSS")] + [(224, 240, "S"), (240, 256, "V")],
+    "prep": [(0, 64), (64, 128), (128, 256)],
+    "sends": [(0, 128), (128, 256)],
+    "fin": [(0, 128), (128, 256)],
+    "calls": ["x", "z", "y"], "lastcalls": ["xz"], "doc2": 4500.0,
+    "gp": 64, "zr0": ("S" * 7 + "V" * 8,) * 2, "zr": ("S" * 6 + "V" * 9, "S" * 6 + "G" * 9), "ssm": "VVVV", "rnd": "SSSS", "clk": "SSSS", "pre": "VVS",
+    "iters": 2000, "seed": 0, "jit": 800.0, "part": 0.1, "heat": 200.0,
+    "cut": 4608, "gc": 1.56, "cy": 0.85, "fix": 0.0, "sfix": 0.0, "pe": 0.43, "pfix": 2.0, "plat": 20.0, "hop": 220.0, "slack": 30.0, "net": 1100.0, "iss": 350.0, "row": 30.0, "rate": 25.0,
 }
 MI = 1 << 20
-XP = 4 * MI
-HI = 4 * MI
-ODD = 6 * MI
+BS = 4 * MI
+HO = 3 * MI
 MAGIC = float(3 << 22)
+WHOLE = float(1 << 23)
 KS = 16512
+KO = 264192
+K0 = (1 << 19) - KO
 
 f32, b16, f16, i32, u16 = "float32", "bfloat16", "float16", "int32", "uint16"
 SCRATCH = {}
@@ -24,39 +30,37 @@ def _sb(dt, shape, *names):
         SCRATCH[n] = ("sbuf", [128] + shape, dt)
 _sb(b16, [W], "doc")
 _sb(b16, [R * 16], "gx", "top", "zrep")
-_sb(i32, [R], "ras", "x0", "y0", "ci", "cp", "kint", "lo")
-_sb(f32, [RO, R], "fs", "xl", "yl", "zs", "zl", "k3")
+_sb(i32, [R], "ras", "x0", "y0", "ci", "cp", "kint", "lo", "a3")
+_sb(f32, [RO, R], "fs", "fy", "xl", "yl", "sp", "zl", "k3", "k1")
 _sb(b16, [RO, R], "us", "ul")
-_sb(f32, [R], "x0f", "y0f", "cf", "rf", "yq", "sp", "t2y", "aa", "uf", "ufl", "kw", "k1", "k2", "k1l", "k2l", "k3l", "kin", "yo")
+_sb(f32, [R], "yr", "zr", "rf", "yq", "t2y", "c1", "e1", "uf", "ufl", "kw", "k1l", "k2l", "k3l", "kf", "kfl", "ks", "ksl", "kin", "yo")
+_sb(f32, [8, R], "hb")
 _sb(u16, [R], "off")
-_sb(b16, [R], "hib", "sg", "ss", "tt", "dl", "ones")
-_sb(f16, [2 * R], "key")
+_sb(b16, [R], "sg", "ss", "sm", "rl", "ones", "ee", "nb")
+_sb(f16, [2 * R], "key", "dg")
 _sb(f16, [8, 2 * R], "pb")
 _sb(i32, [1], "wi", "ti")
 _sb(i32, [8], "pc")
-_sb(b16, [144], "g2")
-_sb(b16, [128], "dt1", "dt2", "in1", "cv")
-_sb(b16, [R], "ee", "nb")
-_sb(i32, [R], "a3")
-_sb(f32, [R], "xm")
 _sb(f32, [32], "col")
-_sb(f32, [8], "cc")
+_sb(f32, [16], "cc")
+_sb(f32, [8], "acc")
 _sb(i32, [16], "i16", "b32", "vi")
-_sb(i32, [RO, 32], "ix")
-_sb(u16, [RO, 32], "iu")
+_sb(i32, [RO, 48], "ix")
+_sb(u16, [RO, 48], "iu")
+_sb(u16, [RO, 16], "un")
 _sb(u16, [16], "pl")
 _sb(f32, [144], "q32")
-_sb(b16, [144], "xf", "t1", "g1", "gw", "ww")
+_sb(b16, [144], "xf", "t1", "g1", "g2", "gw", "ww")
 _sb(f16, [144], "plo", "phi", "qlo", "qhi")
-_sb(f32, [128], "i32m", "sa", "saf", "se", "so", "half")
-_sb(b16, [128], "xh", "gq", "mr", "mh", "dm", "t2", "t3", "t4", "t5", "t6", "bl", "ib", "in128", "xi", "xif", "mx", "my", "ml", "wv", "wvf",
-    "cy", "ca", "caf", "cpm", "cpf", "ch")
-_sb(f16, [128], "ih", "ih128")
+_sb(f32, [128], "se", "so", "half")
+_sb(b16, [128], "xh", "gq", "mr", "mh", "mo", "dm", "t2", "t3", "t4", "t5", "t6", "bl", "ib", "in1", "pr", "xi", "xif", "mx", "my", "ml", "wv", "wvf",
+    "cyl", "ca", "caf", "cpm", "cpf", "ch", "cv", "t7", "sa", "saf", "dt1", "dt2")
+_sb(f16, [128], "ih", "ih128", "ihm")
+_sb(f16, [4, 128], "om")
 _sb(b16, [2 * RO, 128], "al")
-_sb(b16, [2, 512], "ry")
 for _k in range(8):
     SCRATCH["ps%d" % _k] = ("psum", [128, 512], f32)
-SEMAPHORES = ["cV", "cS", "cP", "cG", "snd"] + ["d%d" % _k for _k in range(12)] + ["m%d" % _k for _k in range(32)]
+SEMAPHORES = ["cV", "cS", "cP", "cG", "snd"] + ["d%d" % _k for _k in range(12)] + ["m%d" % _k for _k in range(64)]
 SZ = {f32: 4, i32: 4, b16: 2, f16: 2, u16: 2}
 ALL = slice(None)
 
@@ -67,7 +71,7 @@ def s_(a, b, st=None):
 
 def build(C):
     ops, lastw, readers, bank = [], {}, {}, {}
-    TAILS, GATH, ZS, GC, CY = C["tails"], C["gath"], C["zs"], C["gc"], C["cy"]
+    TAILS, GATH, GC, CY = C["tails"], C["gath"], C["gc"], C["cy"]
 
     def A(name, *idx, p=ALL):
         return (name, idx if idx else (ALL,) * (len(SCRATCH[name][1]) - 1), p)
@@ -89,7 +93,7 @@ def build(C):
             c = cells(a)
             lw = lastw.setdefault(a[0], np.full(int(np.prod(SCRATCH[a[0]][1][1:])), -1))
             for j in np.unique(lw[c]):
-                dep(int(j), not (q == "P" and j >= 0 and ops[int(j)]["q"] == "P"))
+                dep(int(j), not (q == "P" and 0 <= j < k and ops[int(j)]["q"] == "P"))
             keep = []
             for j, m in readers.get(a[0], []):
                 if m[c].any():
@@ -113,7 +117,8 @@ def build(C):
             b["run"].append(k)
         for j in after:
             dep(j, False)
-        ops.append({"q": q, "dur": dur, "lat": lat, "emit": emit, "deps": deps, "kind": kind, "x": extra})
+        tag = (q,) + tuple((a[0], str(a[1][-1])) for a in list(wr) + list(rd))
+        ops.append({"q": q, "dur": dur, "lat": lat, "emit": emit, "deps": deps, "kind": kind, "x": extra, "tag": tag})
         return k
 
     def n_of(a):
@@ -125,37 +130,45 @@ def build(C):
     def vdur(n, c):
         return C["fix"] + max(64, n * c) * CY
 
+    def gdur(n, fix, c=GC):
+        return (fix + n * c) * CY
+
     def isap(x):
         return isinstance(x, tuple)
 
-    def ts(out, in0, s1, op0, s2=None, op1=None, ind=None):
-        rd = [in0] + [x for x in (s1, s2) if isap(x)] + ([ind] if ind else [])
-        c = GC if ind else (0.5 if two(out, in0) else 1)
-        return add("V", vdur(n_of(out), c), ("ts", out, in0, s1, s2, op0, op1, ind), rd, [out])
+    def ts(out, in0, s1, op0, s2=None, op1=None):
+        rd = [in0] + [x for x in (s1, s2) if isap(x)]
+        return add("V", vdur(n_of(out), 0.5 if two(out, in0) else 1), ("ts", out, in0, s1, s2, op0, op1, None), rd, [out])
 
     def tt(out, in0, in1, op, ind=None):
         c = 1 if "ps" in (in0[0][:2], in1[0][:2]) else 2
-        return add("V", vdur(n_of(out), c), ("tt", out, in0, in1, op, ind), [in0, in1] + ([ind] if ind else []), [out])
+        return add("V", gdur(n_of(out), 60, max(GC, 2)) if ind else vdur(n_of(out), c), ("tt", out, in0, in1, op, ind),
+                   [in0, in1] + ([ind] if ind else []), [out])
 
     def cp(out, in_, ind=None, oind=None):
-        c = GC if ind else (3.5 if oind else (0.5 if two(out, in_) else 1))
-        n = n_of(in_) if oind else n_of(out)
-        return add("V", vdur(n, c), ("cp", out, in_, ind, oind), [in_] + [x for x in (ind, oind) if x], [out])
+        dur = gdur(n_of(out), 60) if ind else gdur(n_of(in_), 60, 3.5) if oind else vdur(n_of(out), 0.5 if two(out, in_) else 1)
+        return add("V", dur, ("cp", out, in_, ind, oind), [in_] + [x for x in (ind, oind) if x], [out])
 
     def ms(out, v):
         return add("V", vdur(n_of(out), 0.5 if two(out) else 1), ("ms", out, v), [], [out])
 
     def act(out, in_, fn, bias=0.0, scale=1.0, acc=None, ind=None):
         rd = [in_] + [x for x in (bias, scale) if isap(x)] + ([ind] if ind else [])
-        return add("S", 15 + vdur(n_of(out), GC if ind else 1) + (20 if acc else 0),
+        return add("S", (gdur(n_of(out), 78) if ind else C["sfix"] + vdur(n_of(out), 1)) + (20 if acc else 0),
                    ("act", out, in_, fn, bias, scale, acc, ind), rd, [out] + ([acc] if acc else []))
 
-    def mm(out, lhsT, rhs, start, stop):
-        c = 4 if SCRATCH[rhs[0]][2] == f32 else 1
-        return add("P", 10 + max(64, n_of(rhs)) * c * C["pe"], ("mm", out, lhsT, rhs, start, stop), [lhsT, rhs], [out], lat=60)
+    def mms(l):
+        dur = sum(C["pfix"] + max(64, n_of(x[2])) * (4 if SCRATCH[x[2][0]][2] == f32 else 1) * C["pe"] for x in l)
+        return add("P", dur, ("mm", l), [a for x in l for a in x[1:3]], [x[0] for x in l], lat=C["plat"])
+
+    def mm(*x):
+        return mms([x])
 
     def iota(out, pat, base, cm):
         return add("G", 130 + 2 * n_of(out) * CY, ("iota", out, pat, base, cm), [], [out])
+
+    def gcopy(out, in_):
+        return add("G", 170 + 2 * n_of(out) * CY, ("gcopy", out, in_, n_of(out)), [in_], [out])
 
     nd = [0]
     def load(q, out, src, lat, after=()):
@@ -167,36 +180,41 @@ def build(C):
         return add(q, 60, ("store", dst, src), [src], [], lat=2000, kind="d", extra="d%d" % (nd[0] - 1))
 
     nm = [0]
-    def send(src, dsts):
-        nm[0] += 1
-        sem = "m%d" % (nm[0] - 1)
-        k = add("G", C["iss"], ("send", src, dsts, sem), [src], [], kind="s")
-        by = n_of(src) * SZ[SCRATCH[src[0]][2]]
-        add("R", 0, None, [], [d[1] for d in dsts], lat=C["net"] + len(dsts) * 8 * (40 + by / 16.0), kind="r", after=[k], extra=(sem, 16 * len(dsts)))
+    def send(*trs):
+        sems = ["m%d" % (nm[0] + j) for j in range(len(trs))]
+        nm[0] += len(trs)
+        trs = [(tr[0] if isinstance(tr[0], list) else [tr[0]], tr[1]) for tr in trs]
+        k = add("G", C["iss"], ("send", trs, sems), [x for tr in trs for x in tr[0]], [], kind="s")
+        by = n_of(trs[0][0][0]) * SZ[SCRATCH[trs[0][0][0][0]][2]]
+        dur = max(len(tr[1]) * len(tr[0]) for tr in trs) * 8 * len(trs) * (C["row"] + by / C["rate"])
+        for tr, sem in zip(trs, sems):
+            add("R", dur, None, [], [x[1] for x in tr[1]], lat=C["net"], kind="r", after=[k], extra=(sem, 16 // len(trs) * len(tr[1])))
+            dur = 0.0
         return k
 
     col = lambda k: A("col", s_(k, k + 1))
     cc = lambda k: A("cc", s_(k, k + 1))
     pc = lambda k: A("pc", s_(k, k + 1))
     win = lambda name, sh: A(name, s_(16 - sh, 144 - sh))
-    K33, K65 = slice(0, 33), slice(0, 65)
+    K33, K65, K97, K98 = slice(0, 33), slice(0, 65), slice(0, 97), slice(0, 98)
 
     l1 = load("Y", A("ras"), ("ra", None), 1800)
     l2 = load("S", A("us", 0, ALL), ("zu", None), 1800)
     l3 = load("Y", A("doc", s_(0, C["cut"])), ("xd", (0, C["cut"])), 6000, after=[l1])
     load("S", A("wi"), ("wg", None), 2200, after=[l2])
     load("S", A("ti"), ("th", None), 2200, after=[l2])
-    i1 = iota(pc(0), [[0, 1]], 0, 1)
-    i2 = iota(A("xf"), [[1, 144]], 0, 0)
+    iota(pc(0), [[0, 1]], 0, 1)
+    iota(A("xf"), [[1, 144]], 0, 0)
     for nme, pat in (("xh", [[1, 64], [0, 2]]), ("gq", [[1, 8], [0, 16]]), ("mr", [[0, 8], [1, 16]]), ("i16", [[16, 16]])):
-        i2 = iota(A(nme), pat, 0, 0)
-    s0 = send(A("ras"), [(1, A("x0")), (-1, A("y0"))])
-    s1 = send(A("us", 0, ALL), [(1, A("ul", 0, ALL))])
+        iota(A(nme), pat, 0, 0)
+    s0 = send((A("ras"), [(1, A("x0")), (-1, A("y0"))]))
+    s1 = send((A("us", 0, ALL), [(1, A("ul", 0, ALL))]))
     i3 = add("G", 20, ("inc", "d11"), [], [], kind="i", after=[s0, s1], extra="d11")
-    load("Y", A("doc", s_(C["cut"], W)), ("xd", (C["cut"], W)), 6000, after=[l3])
+    load("Y", A("doc", s_(C["cut"], W)), ("xd", (C["cut"], W)), C["doc2"], after=[l3])
     ops[-1]["deps"][i3] = True
 
     iota(A("mh"), [[0, 8], [1, 8], [0, 2]], 0, 0)
+    iota(A("mo"), [[0, 64], [1, 2]], 0, 0)
     ts(pc(1), pc(0), 0x70, Op.bitwise_and)
     ts(pc(2), pc(0), 15, Op.bitwise_and)
     ts(pc(3), pc(0), 1, Op.bitwise_and)
@@ -205,7 +223,7 @@ def build(C):
     ts(col(15), col(1), 1.0 / 16, Op.mult)
     ts(A("xf"), A("xf"), col(1), Op.subtract)
     ts(A("xh"), A("xh"), col(14), Op.subtract)
-    J, X16 = col(2), A("xf", s_(0, 128))
+    J, ODD, X16 = col(2), col(3), A("xf", s_(0, 128))
     ts(col(4), J, 8.0, Op.is_ge, 500.0, Op.mult)
     ts(col(4), col(4), J, Op.add, 2.0, Op.mult)
     ts(col(5), col(4), 1.0, Op.add)
@@ -213,28 +231,33 @@ def build(C):
     ts(A("so"), X16, col(5), Op.is_equal)
     ts(col(6), J, 14.0, Op.is_ge, 900.0, Op.mult)
     ts(col(6), col(6), J, Op.add, 0.5, Op.mult)
+    ts(col(9), J, 0.5, Op.mult)
     ts(A("sa"), A("xh"), col(6), Op.is_equal)
     ts(A("saf"), X16, col(6), Op.is_equal)
+    ts(A("pr"), A("xh"), col(9), Op.is_equal)
     ts(A("ib"), X16, J, Op.is_equal)
-    for nme, v in (("in128", -128.0), ("xi", float(XP)), ("i32m", 1.0), ("in1", -1.0), ("t3", 512.0)):
+    for k, (nme, v) in enumerate((("sa", 128.0), ("sa", 1.0), ("saf", 128.0), ("saf", 1.0))):
+        ts(A("om", k, ALL), A(nme), v, Op.mult)
+    for nme, v in (("ih", 1.0), ("ih128", 128.0), ("ihm", -128.0)):
+        ts(A(nme), A("ib"), v, Op.mult)
+    for nme, v in (("in1", -1.0), ("t3", 480.0), ("t7", -512.0)):
         act(A(nme), A("ib"), Fn.Copy, scale=v)
-    ts(A("ih"), A("ib"), 1.0, Op.mult)
-    ts(A("ih128"), A("ib"), 128.0, Op.mult)
-    ts(col(7), J, 8.0, Op.is_lt, float(XP), Op.mult)
+    act(A("xi"), A("pr"), Fn.Copy, scale=0.625)
+    ts(col(7), J, 8.0, Op.is_lt, 0.625, Op.mult)
     act(A("xif"), A("ib"), Fn.Identity, scale=col(7))
     for t in range(RO):
-        act(A("al", 2 * t, ALL), A("ib"), Fn.Copy, scale=float((2 * t + 3) << 18))
-        act(A("al", 2 * t + 1, ALL), A("ib"), Fn.Copy, scale=float(-((2 * t + 2) << 18)))
+        act(A("al", 2 * t, ALL), A("pr"), Fn.Copy, scale=(2 * t + 3) / 8.0)
+        act(A("al", 2 * t + 1, ALL), A("pr"), Fn.Copy, scale=-(2 * t + 2) / 8.0)
     ts(A("bl"), A("gq"), col(15), Op.is_equal, 32.0, Op.mult)
     ts(A("dm"), X16, J, Op.subtract)
     ts(A("t2"), A("dm"), -1.0, Op.max, 1.0, Op.min)
-    tt(A("mx"), A("t2"), A("bl"), Op.mult)
-    tt(A("my"), A("bl"), A("t3"), Op.subtract)
-    ts(col(8), col(3), 2.0, Op.mult, -1.0, Op.add)
+    tt(A("t2"), A("t2"), A("bl"), Op.mult)
+    tt(A("mx"), A("t2"), A("t3"), Op.add)
+    tt(A("my"), A("bl"), A("t7"), Op.add)
+    ts(col(8), ODD, BS / 32.0, Op.mult, -BS / 64.0, Op.add)
     act(A("ml"), A("bl"), Fn.Identity, scale=col(8))
-    ts(col(9), col(3), -1.0, Op.mult, 1.0, Op.add)
-    ts(col(18), col(9), float(HI), Op.mult)
-    ts(col(19), col(9), float(-HI - ODD), Op.mult, float(ODD), Op.add)
+    ts(col(19), ODD, 2.0 * HO, Op.mult, float(-HO), Op.add)
+    ts(col(20), J, 64.0, Op.mult, -2048.0 - 63.5 / 128, Op.add)
     ts(A("t1"), A("xf"), 17.0, Op.is_equal)
     ts(A("g1"), A("xf"), 16.0, Op.is_equal)
     tt(A("gw"), A("g1"), A("t1"), Op.subtract)
@@ -243,9 +266,9 @@ def build(C):
     ts(pc(4), A("ti"), 0xFF0, Op.bitwise_and)
     ts(pc(5), A("ti"), 15, Op.bitwise_and)
     ts(col(12), pc(4), -2.0, Op.mult)
-    ts(col(17), pc(5), -2.0, Op.mult, 1.0, Op.add)
+    ts(col(21), pc(5), -2.0, Op.mult, 1.0, Op.add)
     act(A("dt1"), A("ib"), Fn.Identity, scale=col(12))
-    act(A("dt2"), A("ib"), Fn.Identity, scale=col(17))
+    act(A("dt2"), A("ib"), Fn.Identity, scale=col(21))
     tt(A("plo"), A("g1"), A("t1"), Op.add)
     ts(A("phi"), A("plo"), 128.0, Op.mult)
     cp(A("qlo"), A("g1"))
@@ -258,53 +281,64 @@ def build(C):
     act(A("wvf"), win("g1", 7), Fn.Identity, scale=col(11))
     ms(A("ones"), 1.0)
     ms(A("cc"), 0.0)
-    for k, p, v in ((0, 0, 64.0), (1, 0, 320.0), (1, 32, 160.0), (2, 0, 20480.0), (3, 0, -20480.0), (3, 32, -4.25), (4, 0, -245760.0), (4, 32, -1920.0),
-                    (6, 0, -0.5), (6, 32, 2.0 ** -13), (7, 0, -245760.0), (7, 32, -1920.0), (7, 64, float(-MI))):
-        ms(A("cc", s_(k, k + 1), p=slice(p, p + 1)), v)
-    act(A("cy"), A("mr"), Fn.Identity, scale=cc(0), bias=cc(1))
-    ts(A("t4"), A("mr"), 14.0, Op.is_ge)
-    act(A("ca"), A("t4"), Fn.Identity, scale=cc(2), bias=cc(3))
-    act(A("cpm"), A("mh"), Fn.Identity, scale=cc(4), bias=cc(7))
+    rows = {0: (8192.0, 64.0), 1: (-32 * 8192.0, -32 * 64.0),
+            2: (-16384.0, -128.0, -1152.0), 3: (17 * 16384.0, 2048.0, 0.0, -4.25),
+            4: (-245760.0, -1920.0), 5: (241 * 16384.0, 241 * 128.0),
+            6: (-0.5, 2.0 ** -13), 7: (-245760.0, -1920.0, -16.0 * K0), 8: (-245760.0, -1920.0, float(-HO))}
+    ms(A("cc", s_(2, 3), p=slice(96, 98)), float(-HO))
+    ms(A("cc", s_(2, 3), p=slice(96, 97)), 0.0)
+    for k in rows:
+        for p, v in enumerate(rows[k]):
+            if v:
+                ms(A("cc", s_(k, k + 1), p=slice(32 * p, 32 * p + 1)), v)
+    act(A("cyl"), A("mr"), Fn.Identity, scale=cc(0), bias=cc(1))
+    for nme, pat, tmp in (("ca", "mh", "t4"), ("caf", "mr", "t5")):
+        ts(A(tmp, p=slice(0, 64)), A(pat, p=slice(0, 64)), 7.0, Op.min)
+        ts(A(tmp, p=slice(64, 96)), A(pat, p=slice(64, 96)), 7.0, Op.is_ge)
+        cp(A(tmp, p=slice(96, 128)), A("mo", p=slice(96, 128)))
+        act(A(nme), A(tmp), Fn.Identity, scale=cc(2), bias=cc(3))
+    cp(A("mo", p=slice(0, 64)), A("mh", p=slice(0, 64)))
+    act(A("cpm"), A("mo"), Fn.Identity, scale=cc(8), bias=cc(5))
     act(A("cv"), A("ones", s_(0, 128)), Fn.Identity, scale=cc(6))
-    ts(A("t5"), A("mr"), 7.0, Op.is_ge)
-    act(A("caf"), A("t5"), Fn.Identity, scale=cc(2), bias=cc(3))
+    act(A("t6"), A("mr"), Fn.Identity, scale=cc(4), bias=cc(5))
+    ts(A("dm"), A("mr"), 8.0, Op.is_lt)
+    tt(A("cpf"), A("t6"), A("dm"), Op.mult)
     act(A("t6"), A("mr"), Fn.Identity, scale=cc(4), bias=cc(7))
-    ts(A("t5"), A("mr"), 8.0, Op.is_lt)
-    tt(A("cpf"), A("t6"), A("t5"), Op.mult)
-    tt(A("ch"), A("t6"), A("cpf"), Op.subtract)
+    ts(A("dm"), A("mr"), 8.0, Op.is_ge)
+    tt(A("ch"), A("t6"), A("dm"), Op.mult)
     ms(A("half"), 0.5)
-    for c, (a, b) in enumerate(TAILS):
-        w = b - a
-        ms(A("ry", c, s_(0, 3 * w), p=K33), 0.0)
-        ms(A("ry", c, s_(w, 3 * w), p=slice(0, 1)), 1.0)
-        ms(A("ry", c, s_(2 * w, 3 * w), p=slice(32, 33)), 1.0)
     ms(A("zrep", s_(15, 16 * R, 16)), 0.0)
     ts(A("i16"), A("i16"), J, Op.add)
     ts(A("b32"), A("i16"), 32.0, Op.mult)
-    ts(col(13), J, float(KS), Op.mult, float(1 << 18), Op.add)
+    ts(col(13), J, float(KS), Op.mult, float(K0), Op.add)
     ts(A("kin"), A("ras"), col(13), Op.add)
 
-    def c33(name):
-        return A(name, p=K33)
+    def one(K, w):
+        return A("ones", s_(0, w), p=K)
 
     def zrep(t):
+        plan, H = C["zr"] if t else C["zr0"], R // 2
         for k in range(15):
-            if k < ZS:
-                act(A("zrep", s_(k, 16 * R, 16)), A("ul", t, ALL), Fn.Copy)
-            else:
-                cp(A("zrep", s_(k, 16 * R, 16)), A("ul", t, ALL))
+            for a, b, e in ([(0, R, plan[0][k])] if plan[0][k] == plan[1][k] else [(0, H, plan[0][k]), (H, R, plan[1][k])]):
+                o, i = A("zrep", s_(16 * a + k, 16 * b, 16)), A("ul", t, s_(a, b))
+                if e == "S":
+                    act(o, i, Fn.Copy)
+                elif e == "G":
+                    gcopy(o, i)
+                else:
+                    cp(o, i)
 
-    def sign(e, out, in_):
-        if e == "V":
-            ts(out, in_, -1.0, Op.max, 1.0, Op.min)
-        else:
-            act(out, in_, Fn.Sign)
+    def upper(t, a, b, F, S):
+        w = b - a
+        for o, al in ((F, 2 * t), (S, 2 * t + 1)):
+            mms([(o, A("ih128"), A("key", s_(2 * a, 2 * a + w)), True, False), (o, A("ih"), A("key", s_(2 * a + w, 2 * b)), False, False),
+                 (o, A("al", al, ALL), A("sm", s_(a, b)), False, True)])
 
-    cp(A("x0f"), A("x0")); cp(A("y0f"), A("y0"))
-    mm(A("ps6", s_(0, R)), A("se"), A("x0f"), True, False)
-    mm(A("ps6", s_(0, R)), A("so"), A("y0f"), False, True)
-    cp(A("off"), A("ps6", s_(0, R)))
-    ts(A("cf"), A("ps6", s_(0, R)), 20480.0, Op.add)
+    cp(A("zr"), A("x0")); cp(A("yr"), A("y0"))
+    mm(A("ps7", s_(0, R)), A("se"), A("zr"), True, False)
+    mm(A("ps7", s_(0, R)), A("so"), A("yr"), False, True)
+    cp(A("off"), A("ps7", s_(0, R)))
+    cp(A("ci"), A("ps7", s_(0, R)))
     zrep(0)
 
     for t in range(RO):
@@ -312,207 +346,227 @@ def build(C):
         d, d2 = 1 + t % 2, 1 + (t + 1) % 2
         fo = -d if last else d2 - d
         so = 1 if last else 1 + d2
-        unroll = A("iu", t - 1, s_(16, 32)) if t else None
-        for (a, b, e) in GATH:
-            o, ind = A("gx", s_(16 * a, 16 * b)), A("off", s_(a, b))
-            if e == "V":
-                cp(o, A("doc"), ind=ind)
-            else:
-                act(o, A("doc"), Fn.Copy, ind=ind)
-        if C["hib"] == "V":
-            ts(A("hib"), A("cf"), 1.0 / 128, Op.mult, -63.5 / 128, Op.add)
-        else:
-            act(A("hib"), A("cf"), Fn.Identity, bias=-63.5 / 128, scale=1.0 / 128)
         for c, (a, b) in enumerate(TAILS):
-            w = b - a
-            yb, vb = "ps%d" % (2 + c), "ps%d" % (4 + c)
-            mm(A(yb, s_(0, 3 * w)), c33("cy"), A("ry", c, s_(0, 3 * w), p=K33), True, False)
-            mm(A(yb, s_(2 * w, 3 * w)), A("i32m"), A("cf", s_(a, b)), False, False)
-            mm(A(yb, s_(w, 2 * w)), A("ib"), A("hib", s_(a, b)), False, False)
-            mm(A(yb, s_(2 * w, 3 * w)), A("in128"), A("hib", s_(a, b)), False, False)
-            mm(A(vb, s_(w, 2 * w)), c33("caf" if last else "ca"), A("ones", s_(0, w), p=K33), True, False)
-            mm(A(vb, s_(w, 2 * w)), A("saf" if last else "sa"), A("cf", s_(a, b)), False, True)
-        for c, (a, b) in enumerate(TAILS):
-            w = b - a
-            gb, yb, vb, pb = "ps%d" % c, "ps%d" % (2 + c), "ps%d" % (4 + c), "ps%d" % (6 + c)
-            ab = s_(a, b)
-            mm(A(gb, s_(0, w)), A("dt1"), A("ones", s_(0, w)), True, False)
-            mm(A(gb, s_(0, w)), A("dt2"), A("ones", s_(0, w)), False, False)
-            mm(A(pb, s_(340, 340 + w)), A("ib"), A("ul", t, ab), True, True)
+            w, ab = b - a, s_(a, b)
+            def ps(bank, slot):
+                return A("ps%d" % (4 * (c % 2) + bank), s_(128 * slot, 128 * slot + w))
+            G, P21, BA = ps(0, 0), ps(0, 1), ps(0, 2)
+            YL, O, Z, EM, V, ZE, P = ps(1, 3), ps(1, 2), ps(2, 0), ps(2, 1), ps(2, 2), ps(3, 1), ps(3, 0)
+            YH, YO = A(O[0], s_(0, w)), A(O[0], s_(w, 2 * w))
+            E, SG, SM, kh, kl = A("ee", ab), A("sg", ab), A("sm", ab), s_(2 * a, 2 * a + w), s_(2 * a + w, 2 * b)
+            mm(Z, A("ib"), A("ul", t, ab), True, True)
+            mm(ZE, A("ib"), A("ul", t, ab), True, False)
+            ts(A("dg", kh), A("off", ab), 1.0 / 128, Op.mult, col(20), Op.add)
+            mms([(YL, A("cyl", p=K33), one(K33, w), True, False), (YL, A("ihm"), A("dg", kh), False, True)])
+            tt(A("dg", kl), YL, A("ci", ab), Op.add)
+            KA, KP = (K97, K33) if last else (K98, K65)
+            mms([(O, A("caf" if last else "ca", p=KA), one(KA, w), True, False), (O, A("om", 2 * last, ALL), A("dg", kh), False, False),
+                 (O, A("om", 2 * last + 1, ALL), A("dg", kl), False, True)])
+            mm(A(O[0], s_(0, 2 * w)), A("ih"), A("dg", s_(2 * a, 2 * b)), True, False)
+            mms([(G, A("dt1"), one(ALL, w), True, False), (G, A("dt2"), one(ALL, w), False, False)])
             for (a1, b1, e) in GATH:
                 if a <= a1 < b:
                     v = lambda nme: A(nme, s_(16 * a1, 16 * b1))
+                    if e == "V":
+                        cp(v("gx"), A("doc"), ind=A("off", s_(a1, b1)))
+                    else:
+                        act(v("gx"), A("doc"), Fn.Copy, ind=A("off", s_(a1, b1)))
                     add("V", vdur(16 * (b1 - a1), 0.5), ("scan", v("top"), v("gx"), v("zrep")), [v("gx"), v("zrep")], [v("top")])
-                    for k in range(15):
-                        mm(A(gb, s_(a1 - a, b1 - a)), win("gw", k), A("top", s_(16 * a1 + k, 16 * b1, 16)), False, False)
-            E = A("ee", ab)
-            tt(A(pb, s_(170, 170 + w)), A(pb, s_(340, 340 + w)), A("gx", s_(16 * a + 15, 16 * b, 16)), Op.min)
-            tt(E, A(pb, s_(170, 170 + w)), A("top", s_(16 * a + 14, 16 * b, 16)), Op.max)
-            mm(A(gb, s_(0, w)), win("g2", 15), E, False, True)
-            sign(C["clk"][c], A("sg", ab), A(gb, s_(0, w)))
-            mm(A(vb, s_(0, w)), c33("cv"), A("ones", s_(0, w), p=K33), True, False)
-            mm(A(vb, s_(0, w)), A("wvf" if last else "wv"), E, False, True)
-            mm(A(vb, s_(2 * w, 3 * w)), A("ib"), A("ul", t, ab), True, False)
-            mm(A(vb, s_(2 * w, 3 * w)), A("ib"), E, False, True)
-            act(A("uf", ab) if last else A("us", t + 1, ab), A(vb, s_(2 * w, 3 * w)), Fn.Abs, bias=255.0, scale=-1.0)
-            mm(A(yb, s_(0, w)), A("mx"), A("sg", ab), False, False)
-            mm(A(yb, s_(w, 2 * w)), A("my"), A("sg", ab), False, False)
-            mm(A(yb, s_(2 * w, 3 * w)), A("my"), A("sg", ab), False, True)
-            mm(A(gb, s_(2 * w, 3 * w)), A("ml"), A("sg", ab), True, True)
-            sign(C["sgn"][c], A("ss", ab), A(gb, s_(2 * w, 3 * w)))
-            act(A("dl", ab), A("ss", ab), Fn.Identity, bias=float(-MI), scale=float(-8 * MI))
-            act(A("rf", ab), A(vb, s_(0, w)), Fn.Identity, bias=MAGIC)
-            act(A("nb", ab), A("rf", ab), Fn.Identity, bias=-MAGIC)
-            mm(A(vb, s_(0, w)), A("wvf" if last else "wv"), E, True, False)
-            mm(A(vb, s_(0, w)), A("in1"), A("nb", ab), False, True)
-            act(A("yq", ab), A(vb, s_(0, w)), Fn.Square, bias=2.0, scale=1024.0)
-            tt(A("a3", ab), A(vb, s_(w, 2 * w)), A("yq", ab), Op.add)
-            tt(A("tt", ab), A(yb, s_(0, w)), A("sg", ab), Op.mult)
-            kh, kl = s_(2 * a, 2 * a + w), s_(2 * a + w, 2 * b)
-            tt(A("key", kh), A(yb, s_(w, 2 * w)), A("tt", ab), Op.add)
-            tt(A("key", kl), A(yb, s_(2 * w, 3 * w)), A("tt", ab), Op.add)
-            P = A(pb, s_(0, w))
-            mm(P, A("cpf" if last else "cpm", p=K65), A("ones", s_(0, w), p=K65), True, False)
+            for a1 in range(a, b, C["gp"]):
+                b1 = min(b, a1 + C["gp"])
+                for k0 in range(0, 15, 5):
+                    mms([(A(G[0], s_(a1 - a, b1 - a)), win("gw", k), A("top", s_(16 * a1 + k, 16 * b1, 16)), False, False) for k in range(k0, k0 + 5)])
+            tt(EM, Z, A("gx", s_(16 * a + 15, 16 * b, 16)), Op.min)
+            tt(E, EM, A("top", s_(16 * a + 14, 16 * b, 16)), Op.max)
+            mm(G, win("g2", 15), E, False, True)
+            if C["clk"][c] == "V":
+                ts(SG, G, -1.0, Op.max, 1.0, Op.min)
+            else:
+                act(SG, G, Fn.Sign, acc=None if last else A("acc", s_(c, c + 1)))
+            if C["rnd"][c] == "V":
+                mm(V, A("cv", p=K33), one(K33, w), True, False)
+            mm(V, A("wvf" if last else "wv"), E, C["rnd"][c] != "V", True)
+            mm(ZE, A("ib"), E, False, True)
+            mm(P21, A("mx"), SG, True, True)
+            mms([(YH, A("my"), SG, False, False), (YO, A("my"), SG, False, True)])
+            mm(BA, A("ml"), SG, True, True)
+            tt(A("rl", ab), P21, SG, Op.mult)
+            if C["ssm"][c] == "V":
+                ts(SM, BA, float(-BS), Op.max, float(BS), Op.min)
+            else:
+                act(A("ss", ab), BA, Fn.Sign)
+                act(SM, A("ss", ab), Fn.Copy, scale=float(BS))
+            if C["rnd"][c] == "V":
+                ts(A("nb", ab), V, MAGIC, Op.add, MAGIC, Op.subtract)
+            else:
+                act(A("rf", ab), V, Fn.Identity, bias=WHOLE - 0.5, scale=1 + 2.0 ** -21)
+                act(A("nb", ab), A("rf", ab), Fn.Relu, bias=-WHOLE)
+            act(A("uf", ab) if last else A("us", t + 1, ab), ZE, Fn.Abs, bias=255.0, scale=-1.0)
+            mm(V, A("wvf" if last else "wv"), E, True, False)
+            mm(V, A("in1"), A("nb", ab), False, True)
+            act(A("yq", ab), V, Fn.Square, bias=2.0, scale=1024.0)
+            tt(A("key", kh), YH, A("rl", ab), Op.add)
+            tt(A("key", kl), YO, A("rl", ab), Op.add)
+            if last:
+                upper(t, a, b, ps(0, 0), ps(0, 3))
+                act(A("kf", ab), ps(0, 0), Fn.Copy)
+                act(A("ks", ab), ps(0, 3), Fn.Copy)
+            tt(A("a3", ab), O, A("yq", ab), Op.add)
+            mm(P, A("cpf" if last else "cpm", p=KP), one(KP, w), True, False)
+            mm(P, A("xif" if last else "xi"), SM, False, False)
             for j in range(8):
-                ts(A("pb", j, s_(2 * a, 2 * b)), A("key", s_(2 * a, 2 * b)), 128.0 * j, Op.max, 128.0 * (j + 1), Op.min)
-                mm(P, win("qhi", j) if last else win("phi", 2 * j), A("pb", j, kh), False, False)
-                if j == 7:
-                    mm(P, A("xif" if last else "xi"), A("ss", ab), False, False)
-                mm(P, win("qlo", j) if last else win("plo", 2 * j), A("pb", j, kl), False, j == 7)
+                ts(A("pb", j, s_(2 * a, 2 * b)), A("key", s_(2 * a, 2 * b)), 128.0 * j - 2048, Op.max, 128.0 * (j + 1) - 2048, Op.min)
+                mms([(P, win("qhi", j) if last else win("phi", 2 * j), A("pb", j, kh), False, False),
+                     (P, win("qlo", j) if last else win("plo", 2 * j), A("pb", j, kl), False, j == 7)])
             tt(A("fs", t, ab), P, A("a3", ab), Op.max)
-            tt(A("sp", ab) if t else A("zs", t, ab), P, A("dl", ab), Op.add)
+            tt(A("sp", t, ab), P, SM, Op.subtract)
             if c == len(TAILS) - 1:
                 if last:
-                    send(A("uf"), [(fo, A("ufl"))])
+                    send((A("uf"), [(fo, A("ufl"))]))
+                    send((A("kf"), [(fo, A("kfl"))]), (A("ks"), [(so, A("ksl"))]))
                 else:
-                    send(A("us", t + 1, ALL), [(fo, A("ul", t + 1, ALL))])
-        if C["split"] and not last:
-            send(A("fs", t, ALL), [(-d - 1, A("yl", t, ALL))])
-            send(A("fs", t, ALL), [(fo, A("xl", t, ALL))])
-        else:
-            send(A("fs", t, ALL), [(fo, A("xl", t, ALL))] + ([] if last else [(-d - 1, A("yl", t, ALL))]))
-        if t:
-            act(A("zs", t, ALL), A("sp"), Fn.Copy, ind=unroll)
-        send(A("zs", t, ALL), [(so, A("zl", t, ALL))])
-        for kb, al in (("ps2", 2 * t), ("ps3", 2 * t + 1)):
-            for (a, b) in TAILS:
-                w = b - a
-                mm(A(kb, s_(a, b)), A("ih128"), A("key", s_(2 * a, 2 * a + w)), True, False)
-                mm(A(kb, s_(a, b)), A("ih"), A("key", s_(2 * a + w, 2 * b)), False, False)
-                mm(A(kb, s_(a, b)), A("al", al, ALL), A("ss", s_(a, b)), False, True)
-        kacc = A("k1" if d == 1 else "k2")
-        if t < 2:
-            act(kacc, A("ps2", s_(0, R)), Fn.Copy)
-        else:
-            tt(kacc, A("ps2", s_(0, R)), kacc, Op.max)
-        if t == 0:
-            act(A("k3", t, ALL), A("ps3", s_(0, R)), Fn.Copy)
-        else:
-            act(A("kw"), A("ps3", s_(0, R)), Fn.Copy)
-            tt(A("k3", t, ALL), A("kw"), A("k3", t - 1, ALL), Op.max, ind=unroll)
-        if t == RO - 2:
-            send(A("k2"), [(-2, A("k2l"))])
-            tt(A("kin"), A("kin"), A("k2l"), Op.max)
+                    send((A("us", t + 1, ALL), [(fo, A("ul", t + 1, ALL))]))
+            for (a1, b1) in C["sends"]:
+                if b1 == b:
+                    v = lambda nme: A(nme, t, s_(a1, b1))
+                    tr = {"x": (v("fs"), [(fo, v("xl"))]), "y": (v("fy"), [(-d - 1, v("yl"))]), "z": (v("sp"), [(so, v("zl"))])}
+                    if not last:
+                        act(v("fy"), v("fs"), Fn.Identity, scale=ODD, bias=col(19))
+                    for call in (C["lastcalls"] if last else C["calls"]):
+                        send(*[tr[x] for x in call])
         if last:
-            send(A("k1"), [(-1, A("k1l"))])
-            send(A("k3", t, ALL), [(1, A("k3l"))])
             break
-        act(A("tt"), A("sg"), Fn.Copy, acc=col(16))
-        mm(A("ps0", s_(0, 1)), A("half"), col(16), True, True)
-        ts(A("ix", t, s_(0, 16)), A("i16"), A("ps0", s_(0, 1)), Op.add)
-        ts(A("ix", t, s_(16, 32)), A("i16"), A("ps0", s_(0, 1)), Op.subtract)
+        for (a, b) in TAILS:
+            upper(t, a, b, A("ps1", s_(a, b)), A("ps5", s_(a, b)))
+        act(A("k1", t, ALL), A("ps1", s_(0, R)), Fn.Copy)
+        if t == 0:
+            act(A("k3", t, ALL), A("ps5", s_(0, R)), Fn.Copy)
+        else:
+            act(A("kw"), A("ps5", s_(0, R)), Fn.Copy)
+            act(A("k3", t, ALL), A("kw"), Fn.Copy, ind=A("iu", t - 1, s_(16, 32)))
+        if t == 2:
+            send(([A("k1", 0, ALL), A("k1", 2, ALL)], [(-1, A("k1l"))]))
+            tt(A("kin"), A("kin"), A("k1l"), Op.max)
+        if t == 3:
+            send(([A("k1", 1, ALL), A("k1", 3, ALL)], [(-2, A("k2l"))]))
+            send(([A("k3", u, ALL) for u in range(4)], [(1, A("k3l"))]))
+            tt(A("kin"), A("kin"), A("k2l"), Op.max)
+            tt(A("kin"), A("kin"), A("k3l"), Op.max)
+        TU = A("ps6", s_(0, 1))
+        for c, (a, b) in enumerate(TAILS):
+            if C["clk"][c] == "V":
+                act(A("rl", s_(a, b)), A("sg", s_(a, b)), Fn.Copy, acc=A("acc", s_(c, c + 1)))
+        for c in range(len(TAILS)):
+            mm(TU, A("half"), A("acc", s_(c, c + 1)), c == 0, c == len(TAILS) - 1)
+        ts(A("ix", t, s_(0, 16)), A("i16"), TU, Op.add)
+        ts(A("ix", t, s_(16, 32)), A("i16"), TU, Op.subtract)
+        ts(A("ix", t, s_(32, 48)), A("ix", t - 1, s_(16, 32)) if t else A("i16"), TU, Op.add)
         ts(A("ix", t, ALL), A("ix", t, ALL), 255, Op.bitwise_and)
         cp(A("iu", t, ALL), A("ix", t, ALL))
-        for m in range(16):
-            mm(A("ps1", s_(0, 16)), win("ww", m), A("ee", s_(m, R, 16)), m == 0, m == 15)
-        cp(A("vi"), A("ps1", s_(0, 16)))
+        send((A("iu", t, s_(16, 32)), [(1 if t == RO - 2 else 1 + d, A("un", t + 1, ALL))]))
+        for m0 in range(0, 16, 4):
+            mms([(A("ps2", s_(0, 16)), win("ww", m), A("ee", s_(m, R, 16)), m == 0, m == 15) for m in range(m0, m0 + 4)])
+        cp(A("vi"), A("ps2", s_(0, 16)))
         ts(A("vi"), A("vi"), 31, Op.bitwise_and)
         tt(A("vi"), A("vi"), A("b32"), Op.add)
         cp(A("pl"), A("vi"))
         cp(A("doc"), A("ee"), oind=A("pl"))
         zrep(t + 1)
-        act(A("t2y"), A("zs", t, ALL), Fn.Identity, scale=col(3), bias=col(18), ind=A("iu", t, s_(0, 16)))
+        act(A("t2y"), A("sp", t, ALL), Fn.Identity, scale=ODD, bias=col(19), ind=A("iu", t, s_(32, 48)))
         for c, (a, b) in enumerate(C["prep"]):
-            ab = s_(a, b)
-            B = A("ps%d" % (6 + c), s_(0, b - a))
-            tt(A("aa", ab), A("yl", t, ALL), A("t2y", ab), Op.max, ind=A("iu", t, s_(a // 16, b // 16)))
-            act(A("xm", ab), A("xl", t, ab), Fn.Identity, scale=col(9), bias=col(19))
-            tt(B, A("aa", ab), A("xm", ab), Op.add)
-            tt(A("cp", ab), B, A("zl", t, ab), Op.max)
+            ab, roll, un = s_(a, b), A("iu", t, s_(a // 16, b // 16)), A("un", t, s_(a // 16, b // 16))
+            T2, X1, X2 = (A("ps%d" % (4 * (c % 2) + 3), s_(o, o + b - a)) for o in (0, 128, 256))
+            how = C["pre"][c]
+            act(T2, A("t2y", ab), Fn.Copy)
+            if how == "V" and t:
+                tt(A("e1", ab), T2, A("xl", t, ab), Op.max)
+                tt(A("c1", ab), A("zl", t, ALL), A("e1", ab), Op.max, ind=un)
+            else:
+                tt(X1, T2, A("xl", t, ab), Op.max)
+                if t:
+                    act(A("zr", ab), A("zl", t, ALL), Fn.Copy, ind=un)
+                tt(A("c1", ab) if how == "V" else X2, X1, A("zr", ab) if t else A("zl", t, ab), Op.max)
+            if how == "V":
+                tt(A("cp", ab), A("yl", t, ALL), A("c1", ab), Op.max, ind=roll)
+            else:
+                act(A("yr", ab), A("yl", t, ALL), Fn.Copy, ind=roll)
+                tt(A("cp", ab), X2, A("yr", ab), Op.max)
             ts(A("ci", ab), A("cp", ab), 8191, Op.bitwise_and)
             cp(A("off", ab), A("ci", ab))
-        ts(A("cf"), A("ci"), 20480.0, Op.add)
 
     t = RO - 1
-    store("Y", "yz", A("ufl"))
-    tt(A("ps4", s_(0, R)), A("kin"), A("k1l"), Op.max)
-    tt(A("kint"), A("ps4", s_(0, R)), A("k3l"), Op.max)
-    ts(A("kint"), A("kint"), (1 << 18) - 1, Op.bitwise_and)
-    Hh = A("ps5", s_(0, R))
-    mm(Hh, c33("ch"), A("ones", p=K33), True, False)
-    hb = [A("x0f"), A("y0f"), A("cf"), A("rf"), A("t2y"), A("aa"), A("yl", 4, ALL), A("kw")]
-    for j in range(8, 16):
-        ts(hb[j - 8], A("kint"), float(KS * j), Op.max, float(KS * (j + 1)), Op.min)
-        mm(Hh, win("q32", j), hb[j - 8], False, j == 15)
-    tt(A("lo"), A("xl", t, ALL), A("zl", t, ALL), Op.max)
-    ts(A("lo"), A("lo"), 8191, Op.bitwise_and)
-    tt(A("yo"), Hh, A("lo"), Op.add)
-    store("Y", "ya", A("yo"))
+    store("Y", ("yz", (0, R)), A("ufl"))
+    for c, (a, b) in enumerate(C["fin"]):
+        w, ab = b - a, s_(a, b)
+        un = A("un", t, s_(a // 16, b // 16))
+        tt(A("kin", ab), A("kin", ab), A("kfl", ab), Op.max)
+        tt(A("kint", ab), A("ksl"), A("kin", ab), Op.max, ind=un)
+        ts(A("kint", ab), A("kint", ab), (1 << 19) - 1, Op.bitwise_and)
+        Hh = A("ps%d" % (c % 8), s_(0, w))
+        mm(Hh, A("ch", p=K65), one(K65, w), True, False)
+        for j in range(8, 16):
+            ts(A("hb", j - 8, ab), A("kint", ab), float(K0 + KS * j), Op.max, float(K0 + KS * (j + 1)), Op.min)
+            mm(Hh, win("q32", j), A("hb", j - 8, ab), False, j == 15)
+        tt(A("lo", ab), A("zl", t, ALL), A("xl", t, ab), Op.max, ind=un)
+        ts(A("lo", ab), A("lo", ab), 8191, Op.bitwise_and)
+        tt(A("yo", ab), Hh, A("lo", ab), Op.add)
+    store("Y", ("ya", (0, R)), A("yo"))
     return ops
 
 
-def one_pass(ops, pred, succ, pri, C, back):
-    n, hop, slack = len(ops), C["hop"], C["slack"]
-    left = [len(p) for p in pred]
-    free, rdy, fin, st0, order = {}, [0.0] * n, [0.0] * n, [0.0] * n, []
-    cand = {}
-    for k in range(n):
-        if left[k] == 0:
-            cand.setdefault(ops[k]["q"], []).append(k)
-    for _ in range(n):
-        bq, bt = None, 1e30
-        for q, l in cand.items():
-            if l:
-                t = max(min([rdy[j] for j in l]), free.get(q, 0.0) if q != "R" else 0.0)
-                if t < bt:
-                    bq, bt = q, t
-        l = cand[bq]
-        k = max([j for j in l if rdy[j] <= bt + slack], key=lambda j: pri[j])
-        l.remove(k); order.append(k)
-        st0[k] = max(rdy[k], free.get(bq, 0.0) if bq != "R" else 0.0)
-        free[bq] = e = st0[k] + ops[k]["dur"]
-        fin[k] = e + (0.0 if back else ops[k]["lat"])
-        for j, sem in succ[k]:
-            if sem:
-                v = fin[k] + hop + (ops[j]["lat"] if back else 0.0)
-            else:
-                v = e if ops[k if back else j]["q"] == "R" else 0.0
-            rdy[j] = max(rdy[j], v)
-            left[j] -= 1
-            if left[j] == 0:
-                cand.setdefault(ops[j]["q"], []).append(j)
-    return order, max(fin), st0, fin
-
-
 def schedule(ops, C):
-    n = len(ops)
-    pred = [list(o["deps"].items()) for o in ops]
-    succ = [[] for _ in range(n)]
+    n, hop = len(ops), C["hop"]
+    dur, lat, qs = [o["dur"] for o in ops], [o["lat"] for o in ops], [o["q"] for o in ops]
+    fw, bw = [[] for _ in range(n)], [[] for _ in range(n)]
     for k in range(n):
-        for j, sem in pred[k]:
-            succ[j].append((k, sem))
+        for j, sem in ops[k]["deps"].items():
+            d = lat[j] + hop if sem else 0.0
+            fw[j].append((k, d)); bw[k].append((j, d))
+    D, L, idx = np.array(dur), np.array(lat), np.arange(n)
+
+    def one(key, back):
+        succ, eff = bw if back else fw, list(key)
+        for k in (range(n - 1, -1, -1) if back else range(n)):
+            e = eff[k]
+            for j, _d in succ[k]:
+                if eff[j] < e:
+                    eff[j] = e
+        rdy, st, busy = list(lat) if back else [0.0] * n, [0.0] * n, {q: ([], []) for q in set(qs)}
+        for k in np.lexsort((-idx if back else idx, np.array(eff))).tolist():
+            d, t = dur[k], rdy[k]
+            a, b = busy[qs[k]]
+            i = m = len(b)
+            while i and b[i - 1] > t:
+                i -= 1
+            while i < m and a[i] < t + d:
+                if b[i] > t:
+                    t = b[i]
+                i += 1
+            e = t + d
+            a.insert(i, t); b.insert(i, e); st[k] = t
+            for j, w in succ[k]:
+                if e + w > rdy[j]:
+                    rdy[j] = e + w
+        return np.array(st)
+
+    def there_and_back(key):
+        st = one((-(one((-(one(key.tolist(), False) + D)).tolist(), True) + D)).tolist(), False)
+        return float((st + D + L).max()), st
+
     pri = [0.0] * n
     for k in range(n - 1, -1, -1):
-        pri[k] = ops[k]["dur"] + ops[k]["lat"] + max([pri[j] + C["hop"] for j, _s in succ[k]] + [0.0])
-    best = None
-    for _ in range(C["iters"]):
-        order, t, st, fin = one_pass(ops, pred, succ, pri, C, False)
-        if best is None or t < best[1]:
-            best = (order, t, st)
-        pri = one_pass(ops, succ, pred, fin, C, True)[3]
-    for k in range(n):
-        ops[k]["st"] = best[2][k]
-    return best[0], best[1]
+        pri[k] = dur[k] + max([pri[j] + d for j, d in fw[k]] + [lat[k]])
+    names, rng = {}, np.random.default_rng(C["seed"])
+    tag = np.array([names.setdefault(o["tag"], len(names)) for o in ops])
+    cur = best = there_and_back(there_and_back(-np.array(pri))[1])
+    for it in range(C["iters"]):
+        s = C["jit"] * rng.normal(size=len(names)) * (rng.random(len(names)) < C["part"] * rng.random())
+        c = there_and_back(cur[1] + s[tag])
+        if c[0] <= cur[0] + C["heat"] * (1 - it / C["iters"]) * rng.random():
+            cur = c
+        if c[0] < best[0]:
+            best = c
+    return np.lexsort((idx, best[1])).tolist(), best[0]
 
 
 PLAN = []
@@ -579,36 +633,39 @@ def rank_program(g, core, T, topo):
                 kw["accum_out"] = ap(acc)
             ins = g.scalar.activation(ap(out), ap(in_, ind), fn, **kw)
         elif w == "mm":
-            ins = g.tensor.matmul(ap(e[1]), ap(e[2]), ap(e[3]), e[4], e[5])
+            for x in e[1]:
+                ins = g.tensor.matmul(ap(x[0]), ap(x[1]), ap(x[2]), x[3], x[4])
         elif w == "iota":
             if SCRATCH[e[1][0]][2] == i32:
                 ins = g.iota(ap(e[1]), e[2], e[3], e[4])
             else:
                 ins = g.iota(ap(e[1]), e[2], e[3], e[4], allow_small_or_imprecise_dtypes=True)
+        elif w == "gcopy":
+            ins = g.affine_select(ap(e[1]), ap(e[2]), [[0, e[3]]], Op.is_ge, 0.0, 0, 0)
         elif w == "load":
             src = T[e[2][0]][:] if e[2][1] is None else T[e[2][0]][:, e[2][1][0]:e[2][1][1]]
             ins = Q[q].dma_start(ap(e[1]), src)
         elif w == "store":
-            ins = Q[q].dma_start(T[e[1]][:], ap(e[2]))
+            ins = Q[q].dma_start(T[e[1][0]][:, e[1][1][0]:e[1][1][1]], ap(e[2]))
         elif w == "inc":
             g.sem_inc(T.sem[e[1]], 1)
             mark[k] = (e[1], 1); vc[k] = {}
             continue
         else:
-            _, src, dsts, sem = e
-            to = [T.cores[(rank + off) % N] for off, _a in dsts]
-            mask = topo.mask(core, to[0])
-            for c in to[1:]:
-                mask &= topo.mask(core, c)
-            ne = bin(mask).count("1")
-            if len(to) == 1:
-                rid, pid, _s = topo.addr(to[0])
-                g.remote_dma(ap(dsts[0][1]), ap(src), T.sem[sem], T.sem.snd, pid, rid, mask)
+            _, trs, sems = e
+            to = [[T.cores[(rank + off) % N] for off, _a in tr[1]] for tr in trs]
+            eng = [x for x in topo.engines(core, to[0][0]) if all(x in topo.engines(core, c) for l in to for c in l)]
+            ne = len(eng) // len(trs)
+            masks = [sum(1 << x for x in eng[j * ne:(j + 1) * ne]) for j in range(len(trs))]
+            if len(trs) == 1 and len(to[0]) == 1 and len(trs[0][0]) == 1:
+                rid, pid, _s = topo.addr(to[0][0])
+                g.remote_dma(ap(trs[0][1][0][1]), ap(trs[0][0][0]), T.sem[sems[0]], T.sem.snd, pid, rid, masks[0])
             else:
-                ids = [DstId(rid=topo.addr(c)[0], pnc=topo.addr(c)[1]) for c in to]
-                g.remote_dma_fused([RemoteDMATransfer(dst_ids=ids, dma_engine_mask=mask, remote_sem=T.sem[sem], src=ap(src),
-                                                      dsts=[ap(a) for _o, a in dsts])], local_sem=T.sem.snd)
-            sent[0] += ne
+                g.remote_dma_fused([RemoteDMATransfer(dst_ids=[DstId(rid=topo.addr(c)[0], pnc=topo.addr(c)[1]) for c in l], dma_engine_mask=m,
+                                                      remote_sem=T.sem[s], srcs=[ap(x) for x in tr[0]], dsts=[ap(x[1]) for x in tr[1]],
+                                                      alu_op=2 if len(tr[0]) > 1 else 0)
+                                    for tr, l, m, s in zip(trs, to, masks, sems)], local_sem=T.sem.snd)
+            sent[0] += ne * len(trs)
             continue
         if o["kind"] == "d":
             ins.then_inc(T.sem[o["x"]], 16)

import numpy as np
from concourse.bass import DstId, RemoteDMATransfer
from concourse.mybir import AluOpType as Op, ActivationFunctionType as Fn

N, R, W, RO = 4, 256, 8192, 5
CFG = {
    "tails": [(0, 128), (128, 256)],
    "gath": [(32 * _k, 32 * _k + 32, _e) for _k, _e in enumerate("SVSSVSS")] + [(224, 240, "S"), (240, 256, "V")],
    "prep": [(0, 64), (64, 128), (128, 256)],
    "sends": [(0, 128), (128, 256)],
    "fin": [(0, 128), (128, 256)],
    "calls": ["x", "z", "y"], "lastcalls": ["xz"], "doc2": 4500.0,
    "gp": 64, "zr0": ("S" * 7 + "V" * 8,) * 2, "zr": ("S" * 6 + "V" * 9, "S" * 6 + "G" * 9), "ssm": "VVVV", "rnd": "SSSS", "clk": "SSSS", "pre": "VVS",
    "iters": 2000, "seed": 0, "jit": 800.0, "part": 0.1, "heat": 200.0,
    "cut": 4608, "gc": 1.56, "cy": 0.85, "fix": 0.0, "sfix": 0.0, "pe": 0.43, "pfix": 2.0, "plat": 20.0, "hop": 220.0, "slack": 30.0, "net": 1100.0, "iss": 350.0, "row": 30.0, "rate": 25.0,
}
MI = 1 << 20
BS = 4 * MI
HO = 3 * MI
MAGIC = float(3 << 22)
WHOLE = float(1 << 23)
KS = 16512
KO = 264192
K0 = (1 << 19) - KO

f32, b16, f16, i32, u16 = "float32", "bfloat16", "float16", "int32", "uint16"
SCRATCH = {}
def _sb(dt, shape, *names):
    for n in names:
        SCRATCH[n] = ("sbuf", [128] + shape, dt)
_sb(b16, [W], "doc")
_sb(b16, [R * 16], "gx", "top", "zrep")
_sb(i32, [R], "ras", "x0", "y0", "ci", "cp", "kint", "lo", "a3")
_sb(f32, [RO, R], "fs", "fy", "xl", "yl", "sp", "zl", "k3", "k1")
_sb(b16, [RO, R], "us", "ul")
_sb(f32, [R], "yr", "zr", "rf", "yq", "t2y", "c1", "e1", "uf", "ufl", "kw", "k1l", "k2l", "k3l", "kf", "kfl", "ks", "ksl", "kin", "yo")
_sb(f32, [8, R], "hb")
_sb(u16, [R], "off")
_sb(b16, [R], "sg", "ss", "sm", "rl", "ones", "ee", "nb")
_sb(f16, [2 * R], "key", "dg")
_sb(f16, [8, 2 * R], "pb")
_sb(i32, [1], "wi", "ti")
_sb(i32, [8], "pc")
_sb(f32, [32], "col")
_sb(f32, [16], "cc")
_sb(f32, [8], "acc")
_sb(i32, [16], "i16", "b32", "vi")
_sb(i32, [RO, 48], "ix")
_sb(u16, [RO, 48], "iu")
_sb(u16, [RO, 16], "un")
_sb(u16, [16], "pl")
_sb(f32, [144], "q32")
_sb(b16, [144], "xf", "t1", "g1", "g2", "gw", "ww")
_sb(f16, [144], "plo", "phi", "qlo", "qhi")
_sb(f32, [128], "se", "so", "half")
_sb(b16, [128], "xh", "gq", "mr", "mh", "mo", "dm", "t2", "t3", "t4", "t5", "t6", "bl", "ib", "in1", "pr", "xi", "xif", "mx", "my", "ml", "wv", "wvf",
    "cyl", "ca", "caf", "cpm", "cpf", "ch", "cv", "t7", "sa", "saf", "dt1", "dt2")
_sb(f16, [128], "ih", "ih128", "ihm")
_sb(f16, [4, 128], "om")
_sb(b16, [2 * RO, 128], "al")
for _k in range(8):
    SCRATCH["ps%d" % _k] = ("psum", [128, 512], f32)
SEMAPHORES = ["cV", "cS", "cP", "cG", "snd"] + ["d%d" % _k for _k in range(12)] + ["m%d" % _k for _k in range(64)]
SZ = {f32: 4, i32: 4, b16: 2, f16: 2, u16: 2}
ALL = slice(None)


def s_(a, b, st=None):
    return slice(a, b, st)


def build(C):
    ops, lastw, readers, bank = [], {}, {}, {}
    TAILS, GATH, GC, CY = C["tails"], C["gath"], C["gc"], C["cy"]

    def A(name, *idx, p=ALL):
        return (name, idx if idx else (ALL,) * (len(SCRATCH[name][1]) - 1), p)

    def cells(a):
        sh = SCRATCH[a[0]][1][1:]
        return np.arange(int(np.prod(sh))).reshape(sh)[a[1]].reshape(-1)

    def add(q, dur, emit, rd, wr, lat=0.0, kind="c", after=(), extra=None):
        k = len(ops)
        deps = {}
        def dep(j, sem=True):
            if j >= 0 and j != k:
                deps[j] = deps.get(j, False) or sem
        for a in rd:
            for j in np.unique(lastw.setdefault(a[0], np.full(int(np.prod(SCRATCH[a[0]][1][1:])), -1))[cells(a)]):
                dep(int(j))
        for a in wr:
            c = cells(a)
            lw = lastw.setdefault(a[0], np.full(int(np.prod(SCRATCH[a[0]][1][1:])), -1))
            for j in np.unique(lw[c]):
                dep(int(j), not (q == "P" and 0 <= j < k and ops[int(j)]["q"] == "P"))
            keep = []
            for j, m in readers.get(a[0], []):
                if m[c].any():
                    dep(j, not (q == "P" and ops[j]["q"] == "P"))
                    m = m.copy(); m[c] = False
                if m.any():
                    keep.append((j, m))
            readers[a[0]] = keep
            lw[c] = k
        for a in rd:
            m = np.zeros(len(lastw[a[0]]), bool); m[cells(a)] = True
            readers.setdefault(a[0], []).append((k, m))
        for nm in set(a[0] for a in list(rd) + list(wr) if a[0][:2] == "ps"):
            b = bank.setdefault(nm, {"q": None, "run": [], "prev": []})
            if b["q"] != q:
                b["prev"], b["run"], b["q"] = b["run"], [], q
            for j in b["prev"]:
                dep(j)
            if q == "P" and b["run"]:
                dep(b["run"][-1], False)
            b["run"].append(k)
        for j in after:
            dep(j, False)
        tag = (q,) + tuple((a[0], str(a[1][-1])) for a in list(wr) + list(rd))
        ops.append({"q": q, "dur": dur, "lat": lat, "emit": emit, "deps": deps, "kind": kind, "x": extra, "tag": tag})
        return k

    def n_of(a):
        return len(cells(a))

    def two(*aps):
        return all(SZ[SCRATCH[a[0]][2]] == 2 for a in aps)

    def vdur(n, c):
        return C["fix"] + max(64, n * c) * CY

    def gdur(n, fix, c=GC):
        return (fix + n * c) * CY

    def isap(x):
        return isinstance(x, tuple)

    def ts(out, in0, s1, op0, s2=None, op1=None):
        rd = [in0] + [x for x in (s1, s2) if isap(x)]
        return add("V", vdur(n_of(out), 0.5 if two(out, in0) else 1), ("ts", out, in0, s1, s2, op0, op1, None), rd, [out])

    def tt(out, in0, in1, op, ind=None):
        c = 1 if "ps" in (in0[0][:2], in1[0][:2]) else 2
        return add("V", gdur(n_of(out), 60, max(GC, 2)) if ind else vdur(n_of(out), c), ("tt", out, in0, in1, op, ind),
                   [in0, in1] + ([ind] if ind else []), [out])

    def cp(out, in_, ind=None, oind=None):
        dur = gdur(n_of(out), 60) if ind else gdur(n_of(in_), 60, 3.5) if oind else vdur(n_of(out), 0.5 if two(out, in_) else 1)
        return add("V", dur, ("cp", out, in_, ind, oind), [in_] + [x for x in (ind, oind) if x], [out])

    def ms(out, v):
        return add("V", vdur(n_of(out), 0.5 if two(out) else 1), ("ms", out, v), [], [out])

    def act(out, in_, fn, bias=0.0, scale=1.0, acc=None, ind=None):
        rd = [in_] + [x for x in (bias, scale) if isap(x)] + ([ind] if ind else [])
        return add("S", (gdur(n_of(out), 78) if ind else C["sfix"] + vdur(n_of(out), 1)) + (20 if acc else 0),
                   ("act", out, in_, fn, bias, scale, acc, ind), rd, [out] + ([acc] if acc else []))

    def mms(l):
        dur = sum(C["pfix"] + max(64, n_of(x[2])) * (4 if SCRATCH[x[2][0]][2] == f32 else 1) * C["pe"] for x in l)
        return add("P", dur, ("mm", l), [a for x in l for a in x[1:3]], [x[0] for x in l], lat=C["plat"])

    def mm(*x):
        return mms([x])

    def iota(out, pat, base, cm):
        return add("G", 130 + 2 * n_of(out) * CY, ("iota", out, pat, base, cm), [], [out])

    def gcopy(out, in_):
        return add("G", 170 + 2 * n_of(out) * CY, ("gcopy", out, in_, n_of(out)), [in_], [out])

    nd = [0]
    def load(q, out, src, lat, after=()):
        nd[0] += 1
        return add(q, 60, ("load", out, src), [], [out], lat=lat, kind="d", extra="d%d" % (nd[0] - 1), after=after)

    def store(q, dst, src):
        nd[0] += 1
        return add(q, 60, ("store", dst, src), [src], [], lat=2000, kind="d", extra="d%d" % (nd[0] - 1))

    nm = [0]
    def send(*trs):
        sems = ["m%d" % (nm[0] + j) for j in range(len(trs))]
        nm[0] += len(trs)
        trs = [(tr[0] if isinstance(tr[0], list) else [tr[0]], tr[1]) for tr in trs]
        k = add("G", C["iss"], ("send", trs, sems), [x for tr in trs for x in tr[0]], [], kind="s")
        by = n_of(trs[0][0][0]) * SZ[SCRATCH[trs[0][0][0][0]][2]]
        dur = max(len(tr[1]) * len(tr[0]) for tr in trs) * 8 * len(trs) * (C["row"] + by / C["rate"])
        for tr, sem in zip(trs, sems):
            add("R", dur, None, [], [x[1] for x in tr[1]], lat=C["net"], kind="r", after=[k], extra=(sem, 16 // len(trs) * len(tr[1])))
            dur = 0.0
        return k

    col = lambda k: A("col", s_(k, k + 1))
    cc = lambda k: A("cc", s_(k, k + 1))
    pc = lambda k: A("pc", s_(k, k + 1))
    win = lambda name, sh: A(name, s_(16 - sh, 144 - sh))
    K33, K65, K97, K98 = slice(0, 33), slice(0, 65), slice(0, 97), slice(0, 98)

    l1 = load("Y", A("ras"), ("ra", None), 1800)
    l2 = load("S", A("us", 0, ALL), ("zu", None), 1800)
    l3 = load("Y", A("doc", s_(0, C["cut"])), ("xd", (0, C["cut"])), 6000, after=[l1])
    load("S", A("wi"), ("wg", None), 2200, after=[l2])
    load("S", A("ti"), ("th", None), 2200, after=[l2])
    iota(pc(0), [[0, 1]], 0, 1)
    iota(A("xf"), [[1, 144]], 0, 0)
    for nme, pat in (("xh", [[1, 64], [0, 2]]), ("gq", [[1, 8], [0, 16]]), ("mr", [[0, 8], [1, 16]]), ("i16", [[16, 16]])):
        iota(A(nme), pat, 0, 0)
    s0 = send((A("ras"), [(1, A("x0")), (-1, A("y0"))]))
    s1 = send((A("us", 0, ALL), [(1, A("ul", 0, ALL))]))
    i3 = add("G", 20, ("inc", "d11"), [], [], kind="i", after=[s0, s1], extra="d11")
    load("Y", A("doc", s_(C["cut"], W)), ("xd", (C["cut"], W)), C["doc2"], after=[l3])
    ops[-1]["deps"][i3] = True

    iota(A("mh"), [[0, 8], [1, 8], [0, 2]], 0, 0)
    iota(A("mo"), [[0, 64], [1, 2]], 0, 0)
    ts(pc(1), pc(0), 0x70, Op.bitwise_and)
    ts(pc(2), pc(0), 15, Op.bitwise_and)
    ts(pc(3), pc(0), 1, Op.bitwise_and)
    cp(A("col", s_(0, 4)), A("pc", s_(0, 4)))
    ts(col(14), col(1), 0.5, Op.mult)
    ts(col(15), col(1), 1.0 / 16, Op.mult)
    ts(A("xf"), A("xf"), col(1), Op.subtract)
    ts(A("xh"), A("xh"), col(14), Op.subtract)
    J, ODD, X16 = col(2), col(3), A("xf", s_(0, 128))
    ts(col(4), J, 8.0, Op.is_ge, 500.0, Op.mult)
    ts(col(4), col(4), J, Op.add, 2.0, Op.mult)
    ts(col(5), col(4), 1.0, Op.add)
    ts(A("se"), X16, col(4), Op.is_equal)
    ts(A("so"), X16, col(5), Op.is_equal)
    ts(col(6), J, 14.0, Op.is_ge, 900.0, Op.mult)
    ts(col(6), col(6), J, Op.add, 0.5, Op.mult)
    ts(col(9), J, 0.5, Op.mult)
    ts(A("sa"), A("xh"), col(6), Op.is_equal)
    ts(A("saf"), X16, col(6), Op.is_equal)
    ts(A("pr"), A("xh"), col(9), Op.is_equal)
    ts(A("ib"), X16, J, Op.is_equal)
    for k, (nme, v) in enumerate((("sa", 128.0), ("sa", 1.0), ("saf", 128.0), ("saf", 1.0))):
        ts(A("om", k, ALL), A(nme), v, Op.mult)
    for nme, v in (("ih", 1.0), ("ih128", 128.0), ("ihm", -128.0)):
        ts(A(nme), A("ib"), v, Op.mult)
    for nme, v in (("in1", -1.0), ("t3", 480.0), ("t7", -512.0)):
        act(A(nme), A("ib"), Fn.Copy, scale=v)
    act(A("xi"), A("pr"), Fn.Copy, scale=0.625)
    ts(col(7), J, 8.0, Op.is_lt, 0.625, Op.mult)
    act(A("xif"), A("ib"), Fn.Identity, scale=col(7))
    for t in range(RO):
        act(A("al", 2 * t, ALL), A("pr"), Fn.Copy, scale=(2 * t + 3) / 8.0)
        act(A("al", 2 * t + 1, ALL), A("pr"), Fn.Copy, scale=-(2 * t + 2) / 8.0)
    ts(A("bl"), A("gq"), col(15), Op.is_equal, 32.0, Op.mult)
    ts(A("dm"), X16, J, Op.subtract)
    ts(A("t2"), A("dm"), -1.0, Op.max, 1.0, Op.min)
    tt(A("t2"), A("t2"), A("bl"), Op.mult)
    tt(A("mx"), A("t2"), A("t3"), Op.add)
    tt(A("my"), A("bl"), A("t7"), Op.add)
    ts(col(8), ODD, BS / 32.0, Op.mult, -BS / 64.0, Op.add)
    act(A("ml"), A("bl"), Fn.Identity, scale=col(8))
    ts(col(19), ODD, 2.0 * HO, Op.mult, float(-HO), Op.add)
    ts(col(20), J, 64.0, Op.mult, -2048.0 - 63.5 / 128, Op.add)
    ts(A("t1"), A("xf"), 17.0, Op.is_equal)
    ts(A("g1"), A("xf"), 16.0, Op.is_equal)
    tt(A("gw"), A("g1"), A("t1"), Op.subtract)
    ts(A("gw"), A("gw"), 2.0, Op.mult)
    act(A("g2"), A("g1"), Fn.Copy, scale=2.0)
    ts(pc(4), A("ti"), 0xFF0, Op.bitwise_and)
    ts(pc(5), A("ti"), 15, Op.bitwise_and)
    ts(col(12), pc(4), -2.0, Op.mult)
    ts(col(21), pc(5), -2.0, Op.mult, 1.0, Op.add)
    act(A("dt1"), A("ib"), Fn.Identity, scale=col(12))
    act(A("dt2"), A("ib"), Fn.Identity, scale=col(21))
    tt(A("plo"), A("g1"), A("t1"), Op.add)
    ts(A("phi"), A("plo"), 128.0, Op.mult)
    cp(A("qlo"), A("g1"))
    ts(A("qhi"), A("g1"), 128.0, Op.mult)
    act(A("q32"), A("g1"), Fn.Copy)
    cp(col(10), A("wi"))
    ts(col(11), A("wi"), 1.0 / 4096, Op.mult)
    act(A("ww"), A("g1"), Fn.Identity, scale=col(10))
    ts(A("wv"), win("plo", 14), col(11), Op.mult)
    act(A("wvf"), win("g1", 7), Fn.Identity, scale=col(11))
    ms(A("ones"), 1.0)
    ms(A("cc"), 0.0)
    rows = {0: (8192.0, 64.0), 1: (-32 * 8192.0, -32 * 64.0),
            2: (-16384.0, -128.0, -1152.0), 3: (17 * 16384.0, 2048.0, 0.0, -4.25),
            4: (-245760.0, -1920.0), 5: (241 * 16384.0, 241 * 128.0),
            6: (-0.5, 2.0 ** -13), 7: (-245760.0, -1920.0, -16.0 * K0), 8: (-245760.0, -1920.0, float(-HO))}
    ms(A("cc", s_(2, 3), p=slice(96, 98)), float(-HO))
    ms(A("cc", s_(2, 3), p=slice(96, 97)), 0.0)
    for k in rows:
        for p, v in enumerate(rows[k]):
            if v:
                ms(A("cc", s_(k, k + 1), p=slice(32 * p, 32 * p + 1)), v)
    act(A("cyl"), A("mr"), Fn.Identity, scale=cc(0), bias=cc(1))
    for nme, pat, tmp in (("ca", "mh", "t4"), ("caf", "mr", "t5")):
        ts(A(tmp, p=slice(0, 64)), A(pat, p=slice(0, 64)), 7.0, Op.min)
        ts(A(tmp, p=slice(64, 96)), A(pat, p=slice(64, 96)), 7.0, Op.is_ge)
        cp(A(tmp, p=slice(96, 128)), A("mo", p=slice(96, 128)))
        act(A(nme), A(tmp), Fn.Identity, scale=cc(2), bias=cc(3))
    cp(A("mo", p=slice(0, 64)), A("mh", p=slice(0, 64)))
    act(A("cpm"), A("mo"), Fn.Identity, scale=cc(8), bias=cc(5))
    act(A("cv"), A("ones", s_(0, 128)), Fn.Identity, scale=cc(6))
    act(A("t6"), A("mr"), Fn.Identity, scale=cc(4), bias=cc(5))
    ts(A("dm"), A("mr"), 8.0, Op.is_lt)
    tt(A("cpf"), A("t6"), A("dm"), Op.mult)
    act(A("t6"), A("mr"), Fn.Identity, scale=cc(4), bias=cc(7))
    ts(A("dm"), A("mr"), 8.0, Op.is_ge)
    tt(A("ch"), A("t6"), A("dm"), Op.mult)
    ms(A("half"), 0.5)
    ms(A("zrep", s_(15, 16 * R, 16)), 0.0)
    ts(A("i16"), A("i16"), J, Op.add)
    ts(A("b32"), A("i16"), 32.0, Op.mult)
    ts(col(13), J, float(KS), Op.mult, float(K0), Op.add)
    ts(A("kin"), A("ras"), col(13), Op.add)

    def one(K, w):
        return A("ones", s_(0, w), p=K)

    def zrep(t):
        plan, H = C["zr"] if t else C["zr0"], R // 2
        for k in range(15):
            for a, b, e in ([(0, R, plan[0][k])] if plan[0][k] == plan[1][k] else [(0, H, plan[0][k]), (H, R, plan[1][k])]):
                o, i = A("zrep", s_(16 * a + k, 16 * b, 16)), A("ul", t, s_(a, b))
                if e == "S":
                    act(o, i, Fn.Copy)
                elif e == "G":
                    gcopy(o, i)
                else:
                    cp(o, i)

    def upper(t, a, b, F, S):
        w = b - a
        for o, al in ((F, 2 * t), (S, 2 * t + 1)):
            mms([(o, A("ih128"), A("key", s_(2 * a, 2 * a + w)), True, False), (o, A("ih"), A("key", s_(2 * a + w, 2 * b)), False, False),
                 (o, A("al", al, ALL), A("sm", s_(a, b)), False, True)])

    cp(A("zr"), A("x0")); cp(A("yr"), A("y0"))
    mm(A("ps7", s_(0, R)), A("se"), A("zr"), True, False)
    mm(A("ps7", s_(0, R)), A("so"), A("yr"), False, True)
    cp(A("off"), A("ps7", s_(0, R)))
    cp(A("ci"), A("ps7", s_(0, R)))
    zrep(0)

    for t in range(RO):
        last = t == RO - 1
        d, d2 = 1 + t % 2, 1 + (t + 1) % 2
        fo = -d if last else d2 - d
        so = 1 if last else 1 + d2
        for c, (a, b) in enumerate(TAILS):
            w, ab = b - a, s_(a, b)
            def ps(bank, slot):
                return A("ps%d" % (4 * (c % 2) + bank), s_(128 * slot, 128 * slot + w))
            G, P21, BA = ps(0, 0), ps(0, 1), ps(0, 2)
            YL, O, Z, EM, V, ZE, P = ps(1, 3), ps(1, 2), ps(2, 0), ps(2, 1), ps(2, 2), ps(3, 1), ps(3, 0)
            YH, YO = A(O[0], s_(0, w)), A(O[0], s_(w, 2 * w))
            E, SG, SM, kh, kl = A("ee", ab), A("sg", ab), A("sm", ab), s_(2 * a, 2 * a + w), s_(2 * a + w, 2 * b)
            mm(Z, A("ib"), A("ul", t, ab), True, True)
            mm(ZE, A("ib"), A("ul", t, ab), True, False)
            ts(A("dg", kh), A("off", ab), 1.0 / 128, Op.mult, col(20), Op.add)
            mms([(YL, A("cyl", p=K33), one(K33, w), True, False), (YL, A("ihm"), A("dg", kh), False, True)])
            tt(A("dg", kl), YL, A("ci", ab), Op.add)
            KA, KP = (K97, K33) if last else (K98, K65)
            mms([(O, A("caf" if last else "ca", p=KA), one(KA, w), True, False), (O, A("om", 2 * last, ALL), A("dg", kh), False, False),
                 (O, A("om", 2 * last + 1, ALL), A("dg", kl), False, True)])
            mm(A(O[0], s_(0, 2 * w)), A("ih"), A("dg", s_(2 * a, 2 * b)), True, False)
            mms([(G, A("dt1"), one(ALL, w), True, False), (G, A("dt2"), one(ALL, w), False, False)])
            for (a1, b1, e) in GATH:
                if a <= a1 < b:
                    v = lambda nme: A(nme, s_(16 * a1, 16 * b1))
                    if e == "V":
                        cp(v("gx"), A("doc"), ind=A("off", s_(a1, b1)))
                    else:
                        act(v("gx"), A("doc"), Fn.Copy, ind=A("off", s_(a1, b1)))
                    add("V", vdur(16 * (b1 - a1), 0.5), ("scan", v("top"), v("gx"), v("zrep")), [v("gx"), v("zrep")], [v("top")])
            for a1 in range(a, b, C["gp"]):
                b1 = min(b, a1 + C["gp"])
                for k0 in range(0, 15, 5):
                    mms([(A(G[0], s_(a1 - a, b1 - a)), win("gw", k), A("top", s_(16 * a1 + k, 16 * b1, 16)), False, False) for k in range(k0, k0 + 5)])
            tt(EM, Z, A("gx", s_(16 * a + 15, 16 * b, 16)), Op.min)
            tt(E, EM, A("top", s_(16 * a + 14, 16 * b, 16)), Op.max)
            mm(G, win("g2", 15), E, False, True)
            if C["clk"][c] == "V":
                ts(SG, G, -1.0, Op.max, 1.0, Op.min)
            else:
                act(SG, G, Fn.Sign, acc=None if last else A("acc", s_(c, c + 1)))
            if C["rnd"][c] == "V":
                mm(V, A("cv", p=K33), one(K33, w), True, False)
            mm(V, A("wvf" if last else "wv"), E, C["rnd"][c] != "V", True)
            mm(ZE, A("ib"), E, False, True)
            mm(P21, A("mx"), SG, True, True)
            mms([(YH, A("my"), SG, False, False), (YO, A("my"), SG, False, True)])
            mm(BA, A("ml"), SG, True, True)
            tt(A("rl", ab), P21, SG, Op.mult)
            if C["ssm"][c] == "V":
                ts(SM, BA, float(-BS), Op.max, float(BS), Op.min)
            else:
                act(A("ss", ab), BA, Fn.Sign)
                act(SM, A("ss", ab), Fn.Copy, scale=float(BS))
            if C["rnd"][c] == "V":
                ts(A("nb", ab), V, MAGIC, Op.add, MAGIC, Op.subtract)
            else:
                act(A("rf", ab), V, Fn.Identity, bias=WHOLE - 0.5, scale=1 + 2.0 ** -21)
                act(A("nb", ab), A("rf", ab), Fn.Relu, bias=-WHOLE)
            act(A("uf", ab) if last else A("us", t + 1, ab), ZE, Fn.Abs, bias=255.0, scale=-1.0)
            mm(V, A("wvf" if last else "wv"), E, True, False)
            mm(V, A("in1"), A("nb", ab), False, True)
            act(A("yq", ab), V, Fn.Square, bias=2.0, scale=1024.0)
            tt(A("key", kh), YH, A("rl", ab), Op.add)
            tt(A("key", kl), YO, A("rl", ab), Op.add)
            if last:
                upper(t, a, b, ps(0, 0), ps(0, 3))
                act(A("kf", ab), ps(0, 0), Fn.Copy)
                act(A("ks", ab), ps(0, 3), Fn.Copy)
            tt(A("a3", ab), O, A("yq", ab), Op.add)
            mm(P, A("cpf" if last else "cpm", p=KP), one(KP, w), True, False)
            mm(P, A("xif" if last else "xi"), SM, False, False)
            for j in range(8):
                ts(A("pb", j, s_(2 * a, 2 * b)), A("key", s_(2 * a, 2 * b)), 128.0 * j - 2048, Op.max, 128.0 * (j + 1) - 2048, Op.min)
                mms([(P, win("qhi", j) if last else win("phi", 2 * j), A("pb", j, kh), False, False),
                     (P, win("qlo", j) if last else win("plo", 2 * j), A("pb", j, kl), False, j == 7)])
            tt(A("fs", t, ab), P, A("a3", ab), Op.max)
            tt(A("sp", t, ab), P, SM, Op.subtract)
            if c == len(TAILS) - 1:
                if last:
                    send((A("uf"), [(fo, A("ufl"))]))
                    send((A("kf"), [(fo, A("kfl"))]), (A("ks"), [(so, A("ksl"))]))
                else:
                    send((A("us", t + 1, ALL), [(fo, A("ul", t + 1, ALL))]))
            for (a1, b1) in C["sends"]:
                if b1 == b:
                    v = lambda nme: A(nme, t, s_(a1, b1))
                    tr = {"x": (v("fs"), [(fo, v("xl"))]), "y": (v("fy"), [(-d - 1, v("yl"))]), "z": (v("sp"), [(so, v("zl"))])}
                    if not last:
                        act(v("fy"), v("fs"), Fn.Identity, scale=ODD, bias=col(19))
                    for call in (C["lastcalls"] if last else C["calls"]):
                        send(*[tr[x] for x in call])
        if last:
            break
        for (a, b) in TAILS:
            upper(t, a, b, A("ps1", s_(a, b)), A("ps5", s_(a, b)))
        act(A("k1", t, ALL), A("ps1", s_(0, R)), Fn.Copy)
        if t == 0:
            act(A("k3", t, ALL), A("ps5", s_(0, R)), Fn.Copy)
        else:
            act(A("kw"), A("ps5", s_(0, R)), Fn.Copy)
            act(A("k3", t, ALL), A("kw"), Fn.Copy, ind=A("iu", t - 1, s_(16, 32)))
        if t == 2:
            send(([A("k1", 0, ALL), A("k1", 2, ALL)], [(-1, A("k1l"))]))
            tt(A("kin"), A("kin"), A("k1l"), Op.max)
        if t == 3:
            send(([A("k1", 1, ALL), A("k1", 3, ALL)], [(-2, A("k2l"))]))
            send(([A("k3", u, ALL) for u in range(4)], [(1, A("k3l"))]))
            tt(A("kin"), A("kin"), A("k2l"), Op.max)
            tt(A("kin"), A("kin"), A("k3l"), Op.max)
        TU = A("ps6", s_(0, 1))
        for c, (a, b) in enumerate(TAILS):
            if C["clk"][c] == "V":
                act(A("rl", s_(a, b)), A("sg", s_(a, b)), Fn.Copy, acc=A("acc", s_(c, c + 1)))
        for c in range(len(TAILS)):
            mm(TU, A("half"), A("acc", s_(c, c + 1)), c == 0, c == len(TAILS) - 1)
        ts(A("ix", t, s_(0, 16)), A("i16"), TU, Op.add)
        ts(A("ix", t, s_(16, 32)), A("i16"), TU, Op.subtract)
        ts(A("ix", t, s_(32, 48)), A("ix", t - 1, s_(16, 32)) if t else A("i16"), TU, Op.add)
        ts(A("ix", t, ALL), A("ix", t, ALL), 255, Op.bitwise_and)
        cp(A("iu", t, ALL), A("ix", t, ALL))
        send((A("iu", t, s_(16, 32)), [(1 if t == RO - 2 else 1 + d, A("un", t + 1, ALL))]))
        for m0 in range(0, 16, 4):
            mms([(A("ps2", s_(0, 16)), win("ww", m), A("ee", s_(m, R, 16)), m == 0, m == 15) for m in range(m0, m0 + 4)])
        cp(A("vi"), A("ps2", s_(0, 16)))
        ts(A("vi"), A("vi"), 31, Op.bitwise_and)
        tt(A("vi"), A("vi"), A("b32"), Op.add)
        cp(A("pl"), A("vi"))
        cp(A("doc"), A("ee"), oind=A("pl"))
        zrep(t + 1)
        act(A("t2y"), A("sp", t, ALL), Fn.Identity, scale=ODD, bias=col(19), ind=A("iu", t, s_(32, 48)))
        for c, (a, b) in enumerate(C["prep"]):
            ab, roll, un = s_(a, b), A("iu", t, s_(a // 16, b // 16)), A("un", t, s_(a // 16, b // 16))
            T2, X1, X2 = (A("ps%d" % (4 * (c % 2) + 3), s_(o, o + b - a)) for o in (0, 128, 256))
            how = C["pre"][c]
            act(T2, A("t2y", ab), Fn.Copy)
            if how == "V" and t:
                tt(A("e1", ab), T2, A("xl", t, ab), Op.max)
                tt(A("c1", ab), A("zl", t, ALL), A("e1", ab), Op.max, ind=un)
            else:
                tt(X1, T2, A("xl", t, ab), Op.max)
                if t:
                    act(A("zr", ab), A("zl", t, ALL), Fn.Copy, ind=un)
                tt(A("c1", ab) if how == "V" else X2, X1, A("zr", ab) if t else A("zl", t, ab), Op.max)
            if how == "V":
                tt(A("cp", ab), A("yl", t, ALL), A("c1", ab), Op.max, ind=roll)
            else:
                act(A("yr", ab), A("yl", t, ALL), Fn.Copy, ind=roll)
                tt(A("cp", ab), X2, A("yr", ab), Op.max)
            ts(A("ci", ab), A("cp", ab), 8191, Op.bitwise_and)
            cp(A("off", ab), A("ci", ab))

    t = RO - 1
    store("Y", ("yz", (0, R)), A("ufl"))
    for c, (a, b) in enumerate(C["fin"]):
        w, ab = b - a, s_(a, b)
        un = A("un", t, s_(a // 16, b // 16))
        tt(A("kin", ab), A("kin", ab), A("kfl", ab), Op.max)
        tt(A("kint", ab), A("ksl"), A("kin", ab), Op.max, ind=un)
        ts(A("kint", ab), A("kint", ab), (1 << 19) - 1, Op.bitwise_and)
        Hh = A("ps%d" % (c % 8), s_(0, w))
        mm(Hh, A("ch", p=K65), one(K65, w), True, False)
        for j in range(8, 16):
            ts(A("hb", j - 8, ab), A("kint", ab), float(K0 + KS * j), Op.max, float(K0 + KS * (j + 1)), Op.min)
            mm(Hh, win("q32", j), A("hb", j - 8, ab), False, j == 15)
        tt(A("lo", ab), A("zl", t, ALL), A("xl", t, ab), Op.max, ind=un)
        ts(A("lo", ab), A("lo", ab), 8191, Op.bitwise_and)
        tt(A("yo", ab), Hh, A("lo", ab), Op.add)
    store("Y", ("ya", (0, R)), A("yo"))
    return ops


def schedule(ops, C):
    n, hop = len(ops), C["hop"]
    dur, lat, qs = [o["dur"] for o in ops], [o["lat"] for o in ops], [o["q"] for o in ops]
    fw, bw = [[] for _ in range(n)], [[] for _ in range(n)]
    for k in range(n):
        for j, sem in ops[k]["deps"].items():
            d = lat[j] + hop if sem else 0.0
            fw[j].append((k, d)); bw[k].append((j, d))
    D, L, idx = np.array(dur), np.array(lat), np.arange(n)

    def one(key, back):
        succ, eff = bw if back else fw, list(key)
        for k in (range(n - 1, -1, -1) if back else range(n)):
            e = eff[k]
            for j, _d in succ[k]:
                if eff[j] < e:
                    eff[j] = e
        rdy, st, busy = list(lat) if back else [0.0] * n, [0.0] * n, {q: ([], []) for q in set(qs)}
        for k in np.lexsort((-idx if back else idx, np.array(eff))).tolist():
            d, t = dur[k], rdy[k]
            a, b = busy[qs[k]]
            i = m = len(b)
            while i and b[i - 1] > t:
                i -= 1
            while i < m and a[i] < t + d:
                if b[i] > t:
                    t = b[i]
                i += 1
            e = t + d
            a.insert(i, t); b.insert(i, e); st[k] = t
            for j, w in succ[k]:
                if e + w > rdy[j]:
                    rdy[j] = e + w
        return np.array(st)

    def there_and_back(key):
        st = one((-(one((-(one(key.tolist(), False) + D)).tolist(), True) + D)).tolist(), False)
        return float((st + D + L).max()), st

    pri = [0.0] * n
    for k in range(n - 1, -1, -1):
        pri[k] = dur[k] + max([pri[j] + d for j, d in fw[k]] + [lat[k]])
    names, rng = {}, np.random.default_rng(C["seed"])
    tag = np.array([names.setdefault(o["tag"], len(names)) for o in ops])
    cur = best = there_and_back(there_and_back(-np.array(pri))[1])
    for it in range(C["iters"]):
        s = C["jit"] * rng.normal(size=len(names)) * (rng.random(len(names)) < C["part"] * rng.random())
        c = there_and_back(cur[1] + s[tag])
        if c[0] <= cur[0] + C["heat"] * (1 - it / C["iters"]) * rng.random():
            cur = c
        if c[0] < best[0]:
            best = c
    return np.lexsort((idx, best[1])).tolist(), best[0]


PLAN = []


def rank_program(g, core, T, topo):
    rank = T.rank_of(core)
    if rank is None:
        return
    if not PLAN:
        o = build(CFG)
        PLAN.append(o); PLAN.append(schedule(o, CFG)[0])
    ops, order = PLAN
    Q = {"V": g.vector, "S": g.scalar, "P": g.tensor, "G": g, "Y": g.sync}
    need = set(j for o in ops for j, sem in o["deps"].items() if sem)
    count, mark, clock, vc = {}, {}, {q: {} for q in Q}, {}
    sent = [0]

    def ap(a, ind=None):
        v = T[a[0]][(a[2],) + tuple(a[1])]
        return v.indirect(ap(ind)) if ind else v

    def sc(x):
        return ap(x) if isinstance(x, tuple) else x

    def wait(q, sem, n, known):
        if clock[q].get(sem, 0) < n:
            Q[q].wait_ge(T.sem[sem], n)
            clock[q][sem] = n
        for s, v in known.items():
            if clock[q].get(s, 0) < v:
                clock[q][s] = v

    for k in order:
        o = ops[k]
        q, e = o["q"], o["emit"]
        if o["kind"] == "r":
            mark[k] = o["x"]; vc[k] = {}
            continue
        ds = sorted([j for j, sem in o["deps"].items() if sem and ops[j]["kind"] != "s"], key=lambda j: -mark[j][1])
        for j in ds:
            wait(q, mark[j][0], mark[j][1], vc[j])
        w = e[0]
        if w == "ts":
            _, out, in0, s1, s2, op0, op1, ind = e
            ins = g.vector.tensor_scalar(ap(out), ap(in0, ind), sc(s1), sc(s2), op0, op1) if op1 is not None else \
                g.vector.tensor_scalar(ap(out), ap(in0, ind), sc(s1), None, op0)
        elif w == "tt":
            ins = g.vector.tensor_tensor(ap(e[1]), ap(e[2], e[5]), ap(e[3]), e[4])
        elif w == "cp":
            ins = g.vector.tensor_copy(ap(e[1], e[4]), ap(e[2], e[3]))
        elif w == "ms":
            ins = g.vector.memset(ap(e[1]), e[2])
        elif w == "scan":
            ins = g.vector.tensor_tensor_scan(ap(e[1]), ap(e[2]), ap(e[3]), 0.0, Op.max, Op.min)
        elif w == "act":
            _, out, in_, fn, bias, scale, acc, ind = e
            kw = {}
            if isinstance(bias, tuple) or bias != 0.0:
                kw["bias"] = sc(bias)
            if isinstance(scale, tuple) or scale != 1.0:
                kw["scale"] = sc(scale)
            if acc:
                kw["accum_out"] = ap(acc)
            ins = g.scalar.activation(ap(out), ap(in_, ind), fn, **kw)
        elif w == "mm":
            for x in e[1]:
                ins = g.tensor.matmul(ap(x[0]), ap(x[1]), ap(x[2]), x[3], x[4])
        elif w == "iota":
            if SCRATCH[e[1][0]][2] == i32:
                ins = g.iota(ap(e[1]), e[2], e[3], e[4])
            else:
                ins = g.iota(ap(e[1]), e[2], e[3], e[4], allow_small_or_imprecise_dtypes=True)
        elif w == "gcopy":
            ins = g.affine_select(ap(e[1]), ap(e[2]), [[0, e[3]]], Op.is_ge, 0.0, 0, 0)
        elif w == "load":
            src = T[e[2][0]][:] if e[2][1] is None else T[e[2][0]][:, e[2][1][0]:e[2][1][1]]
            ins = Q[q].dma_start(ap(e[1]), src)
        elif w == "store":
            ins = Q[q].dma_start(T[e[1][0]][:, e[1][1][0]:e[1][1][1]], ap(e[2]))
        elif w == "inc":
            g.sem_inc(T.sem[e[1]], 1)
            mark[k] = (e[1], 1); vc[k] = {}
            continue
        else:
            _, trs, sems = e
            to = [[T.cores[(rank + off) % N] for off, _a in tr[1]] for tr in trs]
            eng = [x for x in topo.engines(core, to[0][0]) if all(x in topo.engines(core, c) for l in to for c in l)]
            ne = len(eng) // len(trs)
            masks = [sum(1 << x for x in eng[j * ne:(j + 1) * ne]) for j in range(len(trs))]
            if len(trs) == 1 and len(to[0]) == 1 and len(trs[0][0]) == 1:
                rid, pid, _s = topo.addr(to[0][0])
                g.remote_dma(ap(trs[0][1][0][1]), ap(trs[0][0][0]), T.sem[sems[0]], T.sem.snd, pid, rid, masks[0])
            else:
                g.remote_dma_fused([RemoteDMATransfer(dst_ids=[DstId(rid=topo.addr(c)[0], pnc=topo.addr(c)[1]) for c in l], dma_engine_mask=m,
                                                      remote_sem=T.sem[s], srcs=[ap(x) for x in tr[0]], dsts=[ap(x[1]) for x in tr[1]],
                                                      alu_op=2 if len(tr[0]) > 1 else 0)
                                    for tr, l, m, s in zip(trs, to, masks, sems)], local_sem=T.sem.snd)
            sent[0] += ne * len(trs)
            continue
        if o["kind"] == "d":
            ins.then_inc(T.sem[o["x"]], 16)
            mark[k] = (o["x"], 16)
        elif k in need:
            s = "c" + q
            count[s] = count.get(s, 0) + 1
            ins.then_inc(T.sem[s], 1)
            mark[k] = (s, count[s])
        vc[k] = dict(clock[q])
    for k in mark:
        if ops[k]["kind"] != "c":
            wait("G", mark[k][0], mark[k][1], {})
    for s in count:
        wait("G", s, count[s], {})
    g.wait_ge(T.sem.snd, sent[0])
